import numpy as np
import ml_dtypes


def mxq(x, axis, fmt="e4m3"):
    dtype, down = {"e4m3": (ml_dtypes.float8_e4m3fn, 7), "e5m2": (ml_dtypes.float8_e5m2, 14)}[fmt]
    v = np.moveaxis(np.asarray(x, np.float32).astype(ml_dtypes.bfloat16).astype(np.float64), axis, -1)
    blocks = v.reshape(v.shape[:-1] + (-1, 32))
    amax = np.abs(blocks).max(-1, keepdims=True)
    byte = np.maximum(np.where(amax > 0, np.frexp(amax)[1] - 1 + 127, 0) - down, 1)
    scale = np.exp2(byte - 127.0)
    codes = (blocks / scale).astype(np.float32).astype(dtype).astype(np.float64)
    return np.moveaxis((codes * scale).reshape(v.shape), -1, axis)


WIDE = False


def mx_kscale(k):
    if not WIDE:
        return np.ones(k)
    levels = np.array([10, -10, 5, -5, 0])
    if k % 512:
        return np.exp2(np.random.permutation(np.resize(levels, k // 32))).repeat(32)
    a = np.empty((k // 512, 16))
    for p in range(k // 512):
        a[p, :8] = np.random.permutation(np.resize(levels, 8))
        for g in range(8):
            far = levels[np.abs(levels - a[p, g]) >= 10]
            a[p, g + 8] = far[np.random.randint(len(far))]
    return np.exp2(a.ravel()).repeat(32)


def f64(x):
    return np.asarray(x).astype(np.float64)


def striped(idx):
    return np.tile(idx.reshape(-1, 16).T, (8, 1)).astype(np.uint16)


def unstriped(offs):
    return offs[:16].T.reshape(-1).astype(np.int64)


def pack_weight(w):
    k, n = w.shape
    w = f64(np.asarray(w, np.float32).astype(ml_dtypes.bfloat16)).reshape(k // 32, 32, n)
    amax = np.abs(w).max(1)
    byte = np.clip(np.where(amax > 0, np.frexp(amax)[1] - 1 + 127 - 7, 1), 1, 254)
    scaled = (w * np.exp2(127.0 - byte)[:, None, :]).reshape(k, n).astype(np.float32)
    words = np.ascontiguousarray(scaled.reshape(k // 512, 128, 4, n).transpose(0, 1, 3, 2)).astype(ml_dtypes.float8_e4m3fn).view(np.uint8)
    return words, np.ascontiguousarray(byte.astype(np.uint8).reshape(k // 512, 16, n))


def unpack_weight(words, scales):
    g, p, n, _ = words.shape
    vals = np.ascontiguousarray(words).view(ml_dtypes.float8_e4m3fn).astype(np.float64) * np.repeat(np.exp2(scales.astype(np.float64) - 127.0), 8, axis=1)[..., None]
    return vals.transpose(0, 1, 3, 2).reshape(g * 512, n)


E2M1 = np.array([0.0, 0.5, 1.0, 1.5, 2.0, 3.0, 4.0, 6.0, -0.0, -0.5, -1.0, -1.5, -2.0, -3.0, -4.0, -6.0])


def pack_fp4(w):
    k, n = w.shape
    w = f64(np.asarray(w, np.float32).astype(ml_dtypes.bfloat16)).reshape(k // 32, 32, n)
    amax = np.abs(w).max(1)
    mant, ex = np.frexp(amax / 6.0)
    byte = np.clip(np.where(amax > 0, np.where(mant > 0.5, ex, ex - 1) + 127, 1), 1, 254)
    scaled = (w * np.exp2(127.0 - byte)[:, None, :]).reshape(k, n).astype(np.float32)
    c = np.ascontiguousarray(scaled.reshape(k // 512, 128, 4, n).transpose(0, 1, 3, 2)).astype(ml_dtypes.float4_e2m1fn).view(np.uint8) & 0xF
    words = (c[..., 0::2] | (c[..., 1::2] << 4)).reshape(k // 512, 128, 2 * n)
    return np.ascontiguousarray(words), np.ascontiguousarray(byte.astype(np.uint8).reshape(k // 512, 16, n))


def unpack_fp4(words, scales):
    g, _, n = scales.shape
    words = np.ascontiguousarray(words).reshape(g, 128, n, 2)
    nib = np.empty((g, 128, n, 4), np.uint8)
    nib[..., 0::2] = words & 0xF
    nib[..., 1::2] = words >> 4
    vals = E2M1[nib] * np.repeat(np.exp2(scales.astype(np.float64) - 127.0), 8, axis=1)[..., None]
    return vals.transpose(0, 1, 3, 2).reshape(g * 512, n)


K, T, S, H, N = 1024, 1024, 512, 512, 256


def setup_inputs():
    n = np.random.standard_normal
    s = mx_kscale(K)[:, None]
    u = mx_kscale(H)
    packed_xT = pack_weight(n((K, T)) * s)
    packed_w2 = pack_fp4(n((H, N)) / np.sqrt(H) / u[:, None])
    return {
        "x_words": packed_xT[0],
        "x_scales": packed_xT[1],
        "w1": (n((K, H)) / np.sqrt(K) / s * u).astype(np.float32),
        "w2_words": packed_w2[0],
        "w2_scales": packed_w2[1],
        "pe": (0.5 * n((H, T)) * u[:, None]).astype(np.float32),
        "offs": striped(np.random.permutation(T)[:S]),
    }


def reference(x_words, x_scales, w1, w2_words, w2_scales, pe, offs):
    xq = unpack_weight(x_words, x_scales)[:, unstriped(offs)]
    g = f64(pe)[:, unstriped(offs)]
    h = (mxq(f64(w1), 0, "e4m3").T @ xq) + g
    return unpack_fp4(w2_words, w2_scales).T @ mxq(h, 0, "e4m3")

@@ -1,0 +1,146 @@
+from contextlib import ExitStack
+
+import concourse.mybir as mybir
+
+K, T, S, H, N = 1024, 1024, 512, 512, 256
+FLOPS = 2 * K * H * S + 2 * H * N * S
+
+F32 = mybir.dt.float32
+BF16 = mybir.dt.bfloat16
+I32 = mybir.dt.int32
+U32 = mybir.dt.uint32
+U16 = mybir.dt.uint16
+U8 = mybir.dt.uint8
+FP8X4 = mybir.dt.float8_e4m3fn_x4
+FP4X4 = mybir.dt.float4_e2m1fn_x4
+ADD = mybir.AluOpType.add
+
+P = 128
+PACK = 4
+PASSES = K // (P * PACK)
+HALF = H // 2
+CHUNK = 128
+CHUNKS = S // CHUNK
+
+
+def tile_picked_posadd_none_p_kernel(tc, x_words, x_scales, w1, w2_words, w2_scales, pe, offs, out):
+    nc = tc.nc
+    with ExitStack() as ctx:
+        keep = ctx.enter_context(tc.tile_pool(name="keep", bufs=1))
+        psum = ctx.enter_context(tc.psum_pool(name="psum", bufs=1))
+
+        offsets = keep.tile([P, S // 16], U16, name="offsets")
+        x_table = [keep.tile([P, T], I32, name=f"x_table{z}") for z in range(PASSES)]
+        xs_table = keep.tile([P, T], U8, name="xs_table")
+        w1_raw = [[keep.tile([P, PACK, HALF], F32, name=f"w1_raw{z}{u}") for u in range(2)] for z in range(PASSES)]
+        pe_table = [keep.tile([P, T], F32, name=f"pe_table{t}") for t in range(PACK)]
+        w2_codes = keep.tile([P, 2 * N], U8, name="w2_codes", align_bytes=64)
+        w2_plane = keep.tile([P, N], U8, name="w2_plane", align_bytes=64)
+
+        nc.vector.memset(xs_table[:].bitcast(I32), 0)
+        nc.vector.memset(w2_plane[:].bitcast(I32), 0)
+
+        def load_x(z):
+            nc.sync.dma_start(out=x_table[z][:], in_=x_words[z].rearrange("p c r -> p (c r)").bitcast(I32))
+
+        nc.sync.dma_start(offsets[:], offs)
+        load_x(0)
+        for q in range(4):
+            nc.sync.dma_start(
+                out=xs_table[32 * q : 32 * q + 4 * PASSES, :].bitcast(I32),
+                in_=x_scales[:, 4 * q : 4 * q + 4, :].bitcast(I32),
+            )
+        load_x(1)
+        for z in range(PASSES):
+            for u in range(2):
+                nc.sync.dma_start(
+                    out=w1_raw[z][u][:],
+                    in_=w1[512 * z : 512 * (z + 1), HALF * u : HALF * (u + 1)].rearrange("(p j) c -> p j c", j=PACK),
+                )
+        pe_rows = pe.rearrange("(p t) c -> p t c", t=PACK)
+        for t in range(PACK):
+            nc.sync.dma_start(out=pe_table[t][:], in_=pe_rows[:, t, :])
+        nc.sync.dma_start(out=w2_codes[:].bitcast(I32), in_=w2_words[0].bitcast(I32))
+        for q in range(4):
+            nc.sync.dma_start(
+                out=w2_plane[32 * q : 32 * q + 4, :].bitcast(I32),
+                in_=w2_scales[0, 4 * q : 4 * q + 4, :].bitcast(I32),
+            )
+
+        x_codes = [keep.tile([P, S], U32, name=f"x_codes{z}", align_bytes=64) for z in range(PASSES)]
+        x_planes = keep.tile([P, S], U8, name="x_planes", align_bytes=64)
+        for z in range(PASSES):
+            nc.vector.tensor_copy(x_codes[z][:], x_table[z][:].bitcast(U32).indirect(offsets[:]))
+        nc.vector.tensor_copy(x_planes[:], xs_table[:].indirect(offsets[:]))
+
+        w1_codes = [keep.tile([P, H], U32, name=f"w1_codes{z}", align_bytes=64) for z in range(PASSES)]
+        w1_plane = [keep.tile([P, H], U8, name=f"w1_plane{z}", align_bytes=64) for z in range(PASSES)]
+        for z in range(PASSES):
+            grouped = keep.tile([P, H * PACK], BF16, name=f"w1_grouped{z}", align_bytes=64)
+            dealt = grouped[:].rearrange("p (t m j) -> p m j t", t=PACK, j=PACK)
+            for u in range(2):
+                src = w1_raw[z][u][:].rearrange("p j (m t) -> p m j t", t=PACK)
+                dst = dealt[:, 64 * u : 64 * (u + 1)]
+                if u == 0:
+                    nc.scalar.copy(dst, src)
+                else:
+                    nc.vector.tensor_copy(dst, src)
+            nc.vector.quantize_mx(out=w1_codes[z][:].bitcast(FP8X4), scales=w1_plane[z][:], in_=grouped[:])
+
+        pos = keep.tile([P, PACK, S], F32, name="pos")
+        for t in range(PACK):
+            nc.vector.tensor_copy(pos[:, t, :], pe_table[t][:].indirect(offsets[:]))
+
+        h_bank = [psum.tile([P, PACK, CHUNK], F32, name=f"h_bank{c}") for c in range(CHUNKS)]
+        for c in range(CHUNKS):
+            cols = slice(CHUNK * c, CHUNK * (c + 1))
+            for t in range(PACK):
+                chans = slice(P * t, P * (t + 1))
+                for z in range(PASSES):
+                    nc.tensor.matmul_mx(
+                        out=h_bank[c][:, t, :],
+                        lhsT=w1_codes[z][:, chans].bitcast(FP8X4),
+                        lhsT_scale=w1_plane[z][:, chans],
+                        rhs=x_codes[z][:, cols].bitcast(FP8X4),
+                        rhs_scale=x_planes[4 * z :, cols],
+                        start=(z == 0),
+                        stop=(z == PASSES - 1),
+                    )
+
+        h_bf = [keep.tile([P, CHUNK * PACK], BF16, name=f"h_bf{c}", align_bytes=64) for c in range(CHUNKS)]
+        out_rows = out.rearrange("(a p) n -> p a n", p=P)
+
+        def add_chunk(c):
+            cols = slice(CHUNK * c, CHUNK * (c + 1))
+            nc.vector.tensor_tensor(
+                h_bf[c][:].rearrange("p (b i t) -> p b t i", i=4, t=PACK),
+                h_bank[c][:].rearrange("p t (b i) -> p b t i", i=4),
+                pos[:, :, cols].rearrange("p t (b i) -> p b t i", i=4),
+                ADD,
+            )
+
+        def finish_chunk(c):
+            cols = slice(CHUNK * c, CHUNK * (c + 1))
+            h_codes = keep.tile([P, CHUNK], U32, name=f"h_codes{c}", align_bytes=64)
+            h_plane = keep.tile([P, CHUNK], U8, name=f"h_plane{c}", align_bytes=64)
+            nc.vector.quantize_mx(out=h_codes[:].bitcast(FP8X4), scales=h_plane[:], in_=h_bf[c][:])
+            o_bank = psum.tile([P, N // P, CHUNK], F32, name=f"o_bank{c}")
+            for a in range(N // P):
+                nc.tensor.matmul_mx(
+                    out=o_bank[:, a, :],
+                    lhsT=w2_codes[:, 2 * P * a : 2 * P * (a + 1)].bitcast(FP4X4),
+                    lhsT_scale=w2_plane[:, P * a : P * (a + 1)],
+                    rhs=h_codes[:].bitcast(FP8X4),
+                    rhs_scale=h_plane[:],
+                    start=True,
+                    stop=True,
+                )
+            staged = keep.tile([P, N // P, CHUNK], F32, name=f"staged{c}")
+            nc.scalar.copy(staged[:], o_bank[:])
+            nc.sync.dma_start(out=out_rows[:, :, cols], in_=staged[:])
+
+        add_chunk(0)
+        for c in range(1, CHUNKS):
+            add_chunk(c)
+            finish_chunk(c - 1)
+        finish_chunk(CHUNKS - 1)

@@ -37,29 +37,38 @@ def tile_picked_posadd_none_p_kernel(tc, x_words, x_scales, w1, w2_words, w2_sca
         w2_codes = keep.tile([P, 2 * N], U8, name="w2_codes", align_bytes=64)
         w2_plane = keep.tile([P, N], U8, name="w2_plane", align_bytes=64)
 
-        nc.vector.memset(xs_table[:].bitcast(I32), 0)
-        nc.vector.memset(w2_plane[:].bitcast(I32), 0)
+        nc.gpsimd.memset(xs_table[:].bitcast(I32), 0)
+        nc.gpsimd.memset(w2_plane[:].bitcast(I32), 0)
 
         def load_x(z):
             nc.sync.dma_start(out=x_table[z][:], in_=x_words[z].rearrange("p c r -> p (c r)").bitcast(I32))
 
+        def load_w1(z, u):
+            nc.sync.dma_start(
+                out=w1_raw[z][u][:],
+                in_=w1[512 * z : 512 * (z + 1), HALF * u : HALF * (u + 1)].rearrange("(p j) c -> p j c", j=PACK),
+            )
+
+        pe_rows = pe.rearrange("(p t) c -> p t c", t=PACK)
+
+        def load_pe(t):
+            nc.sync.dma_start(out=pe_table[t][:], in_=pe_rows[:, t, :])
+
         nc.sync.dma_start(offsets[:], offs)
-        load_x(0)
         for q in range(4):
             nc.sync.dma_start(
                 out=xs_table[32 * q : 32 * q + 4 * PASSES, :].bitcast(I32),
                 in_=x_scales[:, 4 * q : 4 * q + 4, :].bitcast(I32),
             )
+        load_w1(0, 0)
+        load_x(0)
+        load_w1(0, 1)
         load_x(1)
-        for z in range(PASSES):
-            for u in range(2):
-                nc.sync.dma_start(
-                    out=w1_raw[z][u][:],
-                    in_=w1[512 * z : 512 * (z + 1), HALF * u : HALF * (u + 1)].rearrange("(p j) c -> p j c", j=PACK),
-                )
-        pe_rows = pe.rearrange("(p t) c -> p t c", t=PACK)
-        for t in range(PACK):
-            nc.sync.dma_start(out=pe_table[t][:], in_=pe_rows[:, t, :])
+        load_w1(1, 0)
+        load_pe(0)
+        load_w1(1, 1)
+        for t in range(1, PACK):
+            load_pe(t)
         nc.sync.dma_start(out=w2_codes[:].bitcast(I32), in_=w2_words[0].bitcast(I32))
         for q in range(4):
             nc.sync.dma_start(
@@ -69,9 +78,9 @@ def tile_picked_posadd_none_p_kernel(tc, x_words, x_scales, w1, w2_words, w2_sca
 
         x_codes = [keep.tile([P, S], U32, name=f"x_codes{z}", align_bytes=64) for z in range(PASSES)]
         x_planes = keep.tile([P, S], U8, name="x_planes", align_bytes=64)
+        nc.vector.tensor_copy(x_planes[:], xs_table[:].indirect(offsets[:]))
         for z in range(PASSES):
             nc.vector.tensor_copy(x_codes[z][:], x_table[z][:].bitcast(U32).indirect(offsets[:]))
-        nc.vector.tensor_copy(x_planes[:], xs_table[:].indirect(offsets[:]))
 
         w1_codes = [keep.tile([P, H], U32, name=f"w1_codes{z}", align_bytes=64) for z in range(PASSES)]
         w1_plane = [keep.tile([P, H], U8, name=f"w1_plane{z}", align_bytes=64) for z in range(PASSES)]
@@ -81,10 +90,7 @@ def tile_picked_posadd_none_p_kernel(tc, x_words, x_scales, w1, w2_words, w2_sca
             for u in range(2):
                 src = w1_raw[z][u][:].rearrange("p j (m t) -> p m j t", t=PACK)
                 dst = dealt[:, 64 * u : 64 * (u + 1)]
-                if u == 0:
-                    nc.scalar.copy(dst, src)
-                else:
-                    nc.vector.tensor_copy(dst, src)
+                nc.scalar.copy(dst, src)
             nc.vector.quantize_mx(out=w1_codes[z][:].bitcast(FP8X4), scales=w1_plane[z][:], in_=grouped[:])
 
         pos = keep.tile([P, PACK, S], F32, name="pos")
@@ -137,7 +143,7 @@ def tile_picked_posadd_none_p_kernel(tc, x_words, x_scales, w1, w2_words, w2_sca
                 )
             staged = keep.tile([P, N // P, CHUNK], F32, name=f"staged{c}")
             nc.scalar.copy(staged[:], o_bank[:])
-            nc.sync.dma_start(out=out_rows[:, :, cols], in_=staged[:])
+            nc.scalar.dma_start(out=out_rows[:, :, cols], in_=staged[:])
 
         add_chunk(0)
         for c in range(1, CHUNKS):

@@ -20,6 +20,7 @@ PACK = 4
 PASSES = K // (P * PACK)
 HALF = H // 2
 CHUNK = 128
+SCALAR_SHARE = 24
 CHUNKS = S // CHUNK
 
 
@@ -32,7 +33,8 @@ def tile_picked_posadd_none_p_kernel(tc, x_words, x_scales, w1, w2_words, w2_sca
         offsets = keep.tile([P, S // 16], U16, name="offsets")
         x_table = [keep.tile([P, T], I32, name=f"x_table{z}") for z in range(PASSES)]
         xs_table = keep.tile([P, T], U8, name="xs_table")
-        w1_raw = [[keep.tile([P, PACK, HALF], F32, name=f"w1_raw{z}{u}") for u in range(2)] for z in range(PASSES)]
+        w1_first = keep.tile([P, PACK, H], F32, name="w1_first")
+        w1_second = [keep.tile([P, PACK, HALF], F32, name=f"w1_second{u}") for u in range(2)]
         pe_table = [keep.tile([P, T], F32, name=f"pe_table{t}") for t in range(PACK)]
         w2_codes = keep.tile([P, 2 * N], U8, name="w2_codes", align_bytes=64)
         w2_plane = keep.tile([P, N], U8, name="w2_plane", align_bytes=64)
@@ -43,11 +45,10 @@ def tile_picked_posadd_none_p_kernel(tc, x_words, x_scales, w1, w2_words, w2_sca
         def load_x(z):
             nc.sync.dma_start(out=x_table[z][:], in_=x_words[z].rearrange("p c r -> p (c r)").bitcast(I32))
 
-        def load_w1(z, u):
-            nc.sync.dma_start(
-                out=w1_raw[z][u][:],
-                in_=w1[512 * z : 512 * (z + 1), HALF * u : HALF * (u + 1)].rearrange("(p j) c -> p j c", j=PACK),
-            )
+        w1_rows = w1.rearrange("(z p j) c -> z p j c", z=PASSES, j=PACK)
+
+        def load_w1_second(u):
+            nc.sync.dma_start(out=w1_second[u][:], in_=w1_rows[1][:, :, HALF * u : HALF * (u + 1)])
 
         pe_rows = pe.rearrange("(p t) c -> p t c", t=PACK)
 
@@ -55,20 +56,20 @@ def tile_picked_posadd_none_p_kernel(tc, x_words, x_scales, w1, w2_words, w2_sca
             nc.sync.dma_start(out=pe_table[t][:], in_=pe_rows[:, t, :])
 
         nc.sync.dma_start(offsets[:], offs)
+        load_x(0)
         for q in range(4):
             nc.sync.dma_start(
                 out=xs_table[32 * q : 32 * q + 4 * PASSES, :].bitcast(I32),
                 in_=x_scales[:, 4 * q : 4 * q + 4, :].bitcast(I32),
             )
-        load_w1(0, 0)
-        load_x(0)
-        load_w1(0, 1)
+        nc.sync.dma_start(out=w1_first[:], in_=w1_rows[0])
         load_x(1)
-        load_w1(1, 0)
         load_pe(0)
-        load_w1(1, 1)
-        for t in range(1, PACK):
-            load_pe(t)
+        load_w1_second(0)
+        load_pe(1)
+        load_w1_second(1)
+        load_pe(2)
+        load_pe(3)
         nc.sync.dma_start(out=w2_codes[:].bitcast(I32), in_=w2_words[0].bitcast(I32))
         for q in range(4):
             nc.sync.dma_start(
@@ -78,24 +79,40 @@ def tile_picked_posadd_none_p_kernel(tc, x_words, x_scales, w1, w2_words, w2_sca
 
         x_codes = [keep.tile([P, S], U32, name=f"x_codes{z}", align_bytes=64) for z in range(PASSES)]
         x_planes = keep.tile([P, S], U8, name="x_planes", align_bytes=64)
-        nc.vector.tensor_copy(x_planes[:], xs_table[:].indirect(offsets[:]))
-        for z in range(PASSES):
-            nc.vector.tensor_copy(x_codes[z][:], x_table[z][:].bitcast(U32).indirect(offsets[:]))
-
         w1_codes = [keep.tile([P, H], U32, name=f"w1_codes{z}", align_bytes=64) for z in range(PASSES)]
         w1_plane = [keep.tile([P, H], U8, name=f"w1_plane{z}", align_bytes=64) for z in range(PASSES)]
-        for z in range(PASSES):
-            grouped = keep.tile([P, H * PACK], BF16, name=f"w1_grouped{z}", align_bytes=64)
-            dealt = grouped[:].rearrange("p (t m j) -> p m j t", t=PACK, j=PACK)
-            for u in range(2):
-                src = w1_raw[z][u][:].rearrange("p j (m t) -> p m j t", t=PACK)
-                dst = dealt[:, 64 * u : 64 * (u + 1)]
-                nc.scalar.copy(dst, src)
-            nc.vector.quantize_mx(out=w1_codes[z][:].bitcast(FP8X4), scales=w1_plane[z][:], in_=grouped[:])
-
+        grouped = [keep.tile([P, H * PACK], BF16, name=f"w1_grouped{z}", align_bytes=64) for z in range(PASSES)]
+        dealt = [tile[:].rearrange("p (t m j) -> p m j t", t=PACK, j=PACK) for tile in grouped]
         pos = keep.tile([P, PACK, S], F32, name="pos")
-        for t in range(PACK):
+
+        def by_channel(raw):
+            return raw[:].rearrange("p j (m t) -> p m j t", t=PACK)
+
+        def pick_x(z):
+            nc.vector.tensor_copy(x_codes[z][:], x_table[z][:].bitcast(U32).indirect(offsets[:]))
+
+        def pick_pe(t):
             nc.vector.tensor_copy(pos[:, t, :], pe_table[t][:].indirect(offsets[:]))
+
+        def quantize_w1(z):
+            nc.vector.quantize_mx(out=w1_codes[z][:].bitcast(FP8X4), scales=w1_plane[z][:], in_=grouped[z][:])
+
+        pick_x(0)
+        nc.vector.tensor_copy(x_planes[:], xs_table[:].indirect(offsets[:]))
+        first = by_channel(w1_first)
+        nc.scalar.copy(dealt[0][:, :64], first[:, :64])
+        nc.vector.tensor_copy(dealt[0][:, 64:], first[:, 64:])
+        pick_x(1)
+        quantize_w1(0)
+        pick_pe(0)
+        nc.scalar.copy(dealt[1][:, :64], by_channel(w1_second[0]))
+        pick_pe(1)
+        last = by_channel(w1_second[1])
+        nc.scalar.copy(dealt[1][:, 64 : 64 + SCALAR_SHARE], last[:, :SCALAR_SHARE])
+        nc.vector.tensor_copy(dealt[1][:, 64 + SCALAR_SHARE :], last[:, SCALAR_SHARE:])
+        quantize_w1(1)
+        pick_pe(2)
+        pick_pe(3)
 
         h_bank = [psum.tile([P, PACK, CHUNK], F32, name=f"h_bank{c}") for c in range(CHUNKS)]
         for c in range(CHUNKS):
@@ -130,10 +147,11 @@ def tile_picked_posadd_none_p_kernel(tc, x_words, x_scales, w1, w2_words, w2_sca
             h_codes = keep.tile([P, CHUNK], U32, name=f"h_codes{c}", align_bytes=64)
             h_plane = keep.tile([P, CHUNK], U8, name=f"h_plane{c}", align_bytes=64)
             nc.vector.quantize_mx(out=h_codes[:].bitcast(FP8X4), scales=h_plane[:], in_=h_bf[c][:])
-            o_bank = psum.tile([P, N // P, CHUNK], F32, name=f"o_bank{c}")
+            staged = keep.tile([P, N // P, CHUNK], F32, name=f"staged{c}")
             for a in range(N // P):
+                o_bank = psum.tile([P, CHUNK], F32, name=f"o_bank{a}", bufs=2)
                 nc.tensor.matmul_mx(
-                    out=o_bank[:, a, :],
+                    out=o_bank[:],
                     lhsT=w2_codes[:, 2 * P * a : 2 * P * (a + 1)].bitcast(FP4X4),
                     lhsT_scale=w2_plane[:, P * a : P * (a + 1)],
                     rhs=h_codes[:].bitcast(FP8X4),
@@ -141,8 +159,10 @@ def tile_picked_posadd_none_p_kernel(tc, x_words, x_scales, w1, w2_words, w2_sca
                     start=True,
                     stop=True,
                 )
-            staged = keep.tile([P, N // P, CHUNK], F32, name=f"staged{c}")
-            nc.scalar.copy(staged[:], o_bank[:])
+                if c == CHUNKS - 1 and a == 0:
+                    nc.vector.tensor_copy(staged[:, a, :], o_bank[:])
+                else:
+                    nc.scalar.copy(staged[:, a, :], o_bank[:])
             nc.scalar.dma_start(out=out_rows[:, :, cols], in_=staged[:])
 
         add_chunk(0)

@@ -20,7 +20,6 @@ PACK = 4
 PASSES = K // (P * PACK)
 HALF = H // 2
 CHUNK = 128
-SCALAR_SHARE = 24
 CHUNKS = S // CHUNK
 
 
@@ -33,41 +32,42 @@ def tile_picked_posadd_none_p_kernel(tc, x_words, x_scales, w1, w2_words, w2_sca
         offsets = keep.tile([P, S // 16], U16, name="offsets")
         x_table = [keep.tile([P, T], I32, name=f"x_table{z}") for z in range(PASSES)]
         xs_table = keep.tile([P, T], U8, name="xs_table")
-        w1_first = keep.tile([P, PACK, H], F32, name="w1_first")
-        w1_second = [keep.tile([P, PACK, HALF], F32, name=f"w1_second{u}") for u in range(2)]
+        w1_raw = [keep.tile([P, PACK, H], F32, name=f"w1_raw{z}") for z in range(PASSES)]
         pe_table = [keep.tile([P, T], F32, name=f"pe_table{t}") for t in range(PACK)]
         w2_codes = keep.tile([P, 2 * N], U8, name="w2_codes", align_bytes=64)
         w2_plane = keep.tile([P, N], U8, name="w2_plane", align_bytes=64)
 
-        nc.gpsimd.memset(xs_table[:].bitcast(I32), 0)
+        nc.vector.memset(xs_table[:].bitcast(I32), 0)
         nc.gpsimd.memset(w2_plane[:].bitcast(I32), 0)
 
         def load_x(z):
             nc.sync.dma_start(out=x_table[z][:], in_=x_words[z].rearrange("p c r -> p (c r)").bitcast(I32))
 
+        def load_x_scales(z):
+            for r in range(4):
+                nc.sync.dma_start(
+                    out=xs_table[4 * z + r : P : 32, :].bitcast(I32),
+                    in_=x_scales[z, r:16:4, :].bitcast(I32),
+                )
+
         w1_rows = w1.rearrange("(z p j) c -> z p j c", z=PASSES, j=PACK)
-
-        def load_w1_second(u):
-            nc.sync.dma_start(out=w1_second[u][:], in_=w1_rows[1][:, :, HALF * u : HALF * (u + 1)])
-
         pe_rows = pe.rearrange("(p t) c -> p t c", t=PACK)
+
+        def load_w1(z):
+            nc.sync.dma_start(out=w1_raw[z][:], in_=w1_rows[z])
 
         def load_pe(t):
             nc.sync.dma_start(out=pe_table[t][:], in_=pe_rows[:, t, :])
 
-        nc.sync.dma_start(offsets[:], offs)
         load_x(0)
-        for q in range(4):
-            nc.sync.dma_start(
-                out=xs_table[32 * q : 32 * q + 4 * PASSES, :].bitcast(I32),
-                in_=x_scales[:, 4 * q : 4 * q + 4, :].bitcast(I32),
-            )
-        nc.sync.dma_start(out=w1_first[:], in_=w1_rows[0])
+        nc.sync.dma_start(offsets[:], offs)
+        load_x_scales(0)
         load_x(1)
         load_pe(0)
-        load_w1_second(0)
+        load_w1(0)
+        load_x_scales(1)
         load_pe(1)
-        load_w1_second(1)
+        load_w1(1)
         load_pe(2)
         load_pe(3)
         nc.sync.dma_start(out=w2_codes[:].bitcast(I32), in_=w2_words[0].bitcast(I32))
@@ -79,56 +79,60 @@ def tile_picked_posadd_none_p_kernel(tc, x_words, x_scales, w1, w2_words, w2_sca
 
         x_codes = [keep.tile([P, S], U32, name=f"x_codes{z}", align_bytes=64) for z in range(PASSES)]
         x_planes = keep.tile([P, S], U8, name="x_planes", align_bytes=64)
-        w1_codes = [keep.tile([P, H], U32, name=f"w1_codes{z}", align_bytes=64) for z in range(PASSES)]
-        w1_plane = [keep.tile([P, H], U8, name=f"w1_plane{z}", align_bytes=64) for z in range(PASSES)]
-        grouped = [keep.tile([P, H * PACK], BF16, name=f"w1_grouped{z}", align_bytes=64) for z in range(PASSES)]
-        dealt = [tile[:].rearrange("p (t m j) -> p m j t", t=PACK, j=PACK) for tile in grouped]
-        pos = keep.tile([P, PACK, S], F32, name="pos")
+        halves = [(z, u) for z in range(PASSES) for u in range(2)]
+        w1_codes = {zu: keep.tile([P, HALF], U32, name="w1_codes%d%d" % zu, align_bytes=64) for zu in halves}
+        w1_plane = {zu: keep.tile([P, HALF], U8, name="w1_plane%d%d" % zu, align_bytes=64) for zu in halves}
+        pos_flat = keep.tile([P, PACK * S], F32, name="pos", align_bytes=64)
+        pos = pos_flat[:].rearrange("p (t s) -> p t s", t=PACK)
+        grouped = {(z, u): pos_flat[:, S * t : S * (t + 1)].bitcast(BF16) for (z, u), t in zip(halves, (1, 2, 2, 3))}
 
-        def by_channel(raw):
-            return raw[:].rearrange("p j (m t) -> p m j t", t=PACK)
+        def round_w1(copy, z, u):
+            copy(
+                grouped[z, u].rearrange("p (t m j) -> p m j t", t=2, j=PACK),
+                w1_raw[z][:].rearrange("p j (m t) -> p m j t", t=PACK)[:, :, :, 2 * u : 2 * u + 2],
+            )
 
         def pick_x(z):
             nc.vector.tensor_copy(x_codes[z][:], x_table[z][:].bitcast(U32).indirect(offsets[:]))
 
         def pick_pe(t):
-            nc.vector.tensor_copy(pos[:, t, :], pe_table[t][:].indirect(offsets[:]))
+            nc.vector.tensor_copy(pos_flat[:, S * t : S * (t + 1)], pe_table[t][:].indirect(offsets[:]))
 
-        def quantize_w1(z):
-            nc.vector.quantize_mx(out=w1_codes[z][:].bitcast(FP8X4), scales=w1_plane[z][:], in_=grouped[z][:])
+        def quantize_w1(z, u):
+            nc.vector.quantize_mx(out=w1_codes[z, u][:].bitcast(FP8X4), scales=w1_plane[z, u][:], in_=grouped[z, u])
 
         pick_x(0)
-        nc.vector.tensor_copy(x_planes[:], xs_table[:].indirect(offsets[:]))
-        first = by_channel(w1_first)
-        nc.scalar.copy(dealt[0][:, :64], first[:, :64])
-        nc.vector.tensor_copy(dealt[0][:, 64:], first[:, 64:])
         pick_x(1)
-        quantize_w1(0)
         pick_pe(0)
-        nc.scalar.copy(dealt[1][:, :64], by_channel(w1_second[0]))
+        round_w1(nc.scalar.copy, 0, 0)
+        round_w1(nc.scalar.copy, 0, 1)
+        nc.vector.tensor_copy(x_planes[:], xs_table[:].indirect(offsets[:]))
+        quantize_w1(0, 0)
         pick_pe(1)
-        last = by_channel(w1_second[1])
-        nc.scalar.copy(dealt[1][:, 64 : 64 + SCALAR_SHARE], last[:, :SCALAR_SHARE])
-        nc.vector.tensor_copy(dealt[1][:, 64 + SCALAR_SHARE :], last[:, SCALAR_SHARE:])
-        quantize_w1(1)
+        quantize_w1(0, 1)
+        round_w1(nc.scalar.copy, 1, 1)
+        round_w1(nc.vector.tensor_copy, 1, 0)
+        quantize_w1(1, 0)
         pick_pe(2)
+        quantize_w1(1, 1)
         pick_pe(3)
 
         h_bank = [psum.tile([P, PACK, CHUNK], F32, name=f"h_bank{c}") for c in range(CHUNKS)]
         for c in range(CHUNKS):
             cols = slice(CHUNK * c, CHUNK * (c + 1))
-            for t in range(PACK):
-                chans = slice(P * t, P * (t + 1))
-                for z in range(PASSES):
-                    nc.tensor.matmul_mx(
-                        out=h_bank[c][:, t, :],
-                        lhsT=w1_codes[z][:, chans].bitcast(FP8X4),
-                        lhsT_scale=w1_plane[z][:, chans],
-                        rhs=x_codes[z][:, cols].bitcast(FP8X4),
-                        rhs_scale=x_planes[4 * z :, cols],
-                        start=(z == 0),
-                        stop=(z == PASSES - 1),
-                    )
+            for u in range(2):
+                for t in range(2):
+                    chans = slice(P * t, P * (t + 1))
+                    for z in range(PASSES):
+                        nc.tensor.matmul_mx(
+                            out=h_bank[c][:, 2 * u + t, :],
+                            lhsT=w1_codes[z, u][:, chans].bitcast(FP8X4),
+                            lhsT_scale=w1_plane[z, u][:, chans],
+                            rhs=x_codes[z][:, cols].bitcast(FP8X4),
+                            rhs_scale=x_planes[4 * z :, cols],
+                            start=(z == 0),
+                            stop=(z == PASSES - 1),
+                        )
 
         h_bf = [keep.tile([P, CHUNK * PACK], BF16, name=f"h_bf{c}", align_bytes=64) for c in range(CHUNKS)]
         out_rows = out.rearrange("(a p) n -> p a n", p=P)
@@ -136,9 +140,9 @@ def tile_picked_posadd_none_p_kernel(tc, x_words, x_scales, w1, w2_words, w2_sca
         def add_chunk(c):
             cols = slice(CHUNK * c, CHUNK * (c + 1))
             nc.vector.tensor_tensor(
-                h_bf[c][:].rearrange("p (b i t) -> p b t i", i=4, t=PACK),
-                h_bank[c][:].rearrange("p t (b i) -> p b t i", i=4),
-                pos[:, :, cols].rearrange("p t (b i) -> p b t i", i=4),
+                h_bf[c][:].rearrange("p (b i t) -> p b t i", i=2, t=PACK),
+                h_bank[c][:].rearrange("p t (b i) -> p b t i", i=2),
+                pos[:, :, cols].rearrange("p t (b i) -> p b t i", i=2),
                 ADD,
             )
 

@@ -32,7 +32,8 @@ def tile_picked_posadd_none_p_kernel(tc, x_words, x_scales, w1, w2_words, w2_sca
         offsets = keep.tile([P, S // 16], U16, name="offsets")
         x_table = [keep.tile([P, T], I32, name=f"x_table{z}") for z in range(PASSES)]
         xs_table = keep.tile([P, T], U8, name="xs_table")
-        w1_raw = [keep.tile([P, PACK, H], F32, name=f"w1_raw{z}") for z in range(PASSES)]
+        w1_first = keep.tile([P, PACK, H], F32, name="w1_first")
+        w1_second = [keep.tile([P, PACK, HALF], F32, name=f"w1_second{v}") for v in range(2)]
         pe_table = [keep.tile([P, T], F32, name=f"pe_table{t}") for t in range(PACK)]
         w2_codes = keep.tile([P, 2 * N], U8, name="w2_codes", align_bytes=64)
         w2_plane = keep.tile([P, N], U8, name="w2_plane", align_bytes=64)
@@ -43,33 +44,22 @@ def tile_picked_posadd_none_p_kernel(tc, x_words, x_scales, w1, w2_words, w2_sca
         def load_x(z):
             nc.sync.dma_start(out=x_table[z][:], in_=x_words[z].rearrange("p c r -> p (c r)").bitcast(I32))
 
-        def load_x_scales(z):
-            for r in range(4):
-                nc.sync.dma_start(
-                    out=xs_table[4 * z + r : P : 32, :].bitcast(I32),
-                    in_=x_scales[z, r:16:4, :].bitcast(I32),
-                )
-
         w1_rows = w1.rearrange("(z p j) c -> z p j c", z=PASSES, j=PACK)
         pe_rows = pe.rearrange("(p t) c -> p t c", t=PACK)
 
-        def load_w1(z):
-            nc.sync.dma_start(out=w1_raw[z][:], in_=w1_rows[z])
-
-        def load_pe(t):
-            nc.sync.dma_start(out=pe_table[t][:], in_=pe_rows[:, t, :])
-
         load_x(0)
         nc.sync.dma_start(offsets[:], offs)
-        load_x_scales(0)
+        for q in range(4):
+            nc.sync.dma_start(
+                out=xs_table[32 * q : 32 * q + 4 * PASSES, :].bitcast(I32),
+                in_=x_scales[:, 4 * q : 4 * q + 4, :].bitcast(I32),
+            )
         load_x(1)
-        load_pe(0)
-        load_w1(0)
-        load_x_scales(1)
-        load_pe(1)
-        load_w1(1)
-        load_pe(2)
-        load_pe(3)
+        nc.sync.dma_start(out=w1_first[:], in_=w1_rows[0])
+        for v in range(2):
+            nc.sync.dma_start(out=w1_second[v][:], in_=w1_rows[1][:, :, HALF * v : HALF * (v + 1)])
+        for t in range(PACK):
+            nc.sync.dma_start(out=pe_table[t][:], in_=pe_rows[:, t, :])
         nc.sync.dma_start(out=w2_codes[:].bitcast(I32), in_=w2_words[0].bitcast(I32))
         for q in range(4):
             nc.sync.dma_start(
@@ -82,80 +72,89 @@ def tile_picked_posadd_none_p_kernel(tc, x_words, x_scales, w1, w2_words, w2_sca
         halves = [(z, u) for z in range(PASSES) for u in range(2)]
         w1_codes = {zu: keep.tile([P, HALF], U32, name="w1_codes%d%d" % zu, align_bytes=64) for zu in halves}
         w1_plane = {zu: keep.tile([P, HALF], U8, name="w1_plane%d%d" % zu, align_bytes=64) for zu in halves}
-        pos_flat = keep.tile([P, PACK * S], F32, name="pos", align_bytes=64)
-        pos = pos_flat[:].rearrange("p (t s) -> p t s", t=PACK)
-        grouped = {(z, u): pos_flat[:, S * t : S * (t + 1)].bitcast(BF16) for (z, u), t in zip(halves, (1, 2, 2, 3))}
+        pos_first = keep.tile([P, S], F32, name="pos_first", align_bytes=64)
+        grouped = {zu: keep.tile([P, HALF * PACK], BF16, name="grouped%d%d" % zu, align_bytes=64)[:] for zu in halves[:3]}
+        grouped[1, 1] = pos_first[:].bitcast(BF16)
+        h_sum = keep.tile([P, PACK * S], F32, name="h_sum")
+        h_bank = [psum.tile([P, S], F32, name=f"h_bank{t}") for t in range(PACK)]
 
-        def round_w1(copy, z, u):
-            copy(
-                grouped[z, u].rearrange("p (t m j) -> p m j t", t=2, j=PACK),
-                w1_raw[z][:].rearrange("p j (m t) -> p m j t", t=PACK)[:, :, :, 2 * u : 2 * u + 2],
-            )
+        def round_w1(z, raw, groups):
+            for u, copy in ((1, nc.scalar.copy), (0, nc.vector.tensor_copy)):
+                copy(
+                    grouped[z, u].rearrange("p (t m j) -> p m j t", t=2, j=PACK)[:, groups],
+                    raw[:].rearrange("p j (m t) -> p m j t", t=PACK)[:, :, :, 2 * u : 2 * u + 2],
+                )
 
         def pick_x(z):
             nc.vector.tensor_copy(x_codes[z][:], x_table[z][:].bitcast(U32).indirect(offsets[:]))
 
-        def pick_pe(t):
-            nc.vector.tensor_copy(pos_flat[:, S * t : S * (t + 1)], pe_table[t][:].indirect(offsets[:]))
-
         def quantize_w1(z, u):
             nc.vector.quantize_mx(out=w1_codes[z, u][:].bitcast(FP8X4), scales=w1_plane[z, u][:], in_=grouped[z, u])
 
+        def multiply(z, u):
+            for t in (1, 0) if u == 0 else (0, 1):
+                chans = slice(P * t, P * (t + 1))
+                nc.tensor.matmul_mx(
+                    out=h_bank[2 * u + t][:],
+                    lhsT=w1_codes[z, u][:, chans].bitcast(FP8X4),
+                    lhsT_scale=w1_plane[z, u][:, chans],
+                    rhs=x_codes[z][:].bitcast(FP8X4),
+                    rhs_scale=x_planes[4 * z :, :],
+                    start=(z == 0),
+                    stop=(z == PASSES - 1),
+                )
+
         pick_x(0)
         pick_x(1)
-        pick_pe(0)
-        round_w1(nc.scalar.copy, 0, 0)
-        round_w1(nc.scalar.copy, 0, 1)
         nc.vector.tensor_copy(x_planes[:], xs_table[:].indirect(offsets[:]))
-        quantize_w1(0, 0)
-        pick_pe(1)
-        quantize_w1(0, 1)
-        round_w1(nc.scalar.copy, 1, 1)
-        round_w1(nc.vector.tensor_copy, 1, 0)
-        quantize_w1(1, 0)
-        pick_pe(2)
-        quantize_w1(1, 1)
-        pick_pe(3)
+        round_w1(0, w1_first, slice(0, P))
+        for u in range(2):
+            quantize_w1(0, u)
+            multiply(0, u)
+        for v in range(2):
+            round_w1(1, w1_second[v], slice(64 * v, 64 * (v + 1)))
+        for u in range(2):
+            quantize_w1(1, u)
+            multiply(1, u)
+        nc.vector.tensor_copy(pos_first[:], pe_table[0][:].indirect(offsets[:]))
 
-        h_bank = [psum.tile([P, PACK, CHUNK], F32, name=f"h_bank{c}") for c in range(CHUNKS)]
-        for c in range(CHUNKS):
-            cols = slice(CHUNK * c, CHUNK * (c + 1))
-            for u in range(2):
-                for t in range(2):
-                    chans = slice(P * t, P * (t + 1))
-                    for z in range(PASSES):
-                        nc.tensor.matmul_mx(
-                            out=h_bank[c][:, 2 * u + t, :],
-                            lhsT=w1_codes[z, u][:, chans].bitcast(FP8X4),
-                            lhsT_scale=w1_plane[z, u][:, chans],
-                            rhs=x_codes[z][:, cols].bitcast(FP8X4),
-                            rhs_scale=x_planes[4 * z :, cols],
-                            start=(z == 0),
-                            stop=(z == PASSES - 1),
-                        )
+        product = [keep.tile([P, S], F32, name=f"product{t}") for t in range(1, PACK)]
+        for t in range(1, PACK):
+            nc.scalar.copy(product[t - 1][:], h_bank[t][:])
+        nc.vector.tensor_tensor(h_sum[:, 0:S], h_bank[0][:], pos_first[:], ADD)
+        for t in range(1, PACK - 1):
+            nc.vector.tensor_tensor(h_sum[:, S * t : S * (t + 1)], pe_table[t][:].indirect(offsets[:]), product[t - 1][:], ADD)
 
-        h_bf = [keep.tile([P, CHUNK * PACK], BF16, name=f"h_bf{c}", align_bytes=64) for c in range(CHUNKS)]
+        h_bf = keep.tile([P, S * PACK], BF16, name="h_bf", align_bytes=64)
+        woven = h_bf[:].rearrange("p (b i t) -> p b t i", i=2, t=PACK)
+        planes = h_sum[:].rearrange("p (t b i) -> p b t i", i=2, t=PACK)
+        nc.scalar.copy(woven[:, :, 0:2, :], planes[:, :, 0:2, :])
         out_rows = out.rearrange("(a p) n -> p a n", p=P)
 
-        def add_chunk(c):
+        def sum_last(c):
             cols = slice(CHUNK * c, CHUNK * (c + 1))
             nc.vector.tensor_tensor(
-                h_bf[c][:].rearrange("p (b i t) -> p b t i", i=2, t=PACK),
-                h_bank[c][:].rearrange("p t (b i) -> p b t i", i=2),
-                pos[:, :, cols].rearrange("p t (b i) -> p b t i", i=2),
+                h_sum[:, 3 * S + CHUNK * c : 3 * S + CHUNK * (c + 1)],
+                pe_table[3][:].indirect(offsets[:, CHUNK * c // 16 : CHUNK * (c + 1) // 16]),
+                product[2][:, cols],
                 ADD,
             )
+            pairs = slice(CHUNK * c // 2, CHUNK * (c + 1) // 2)
+            nc.scalar.copy(woven[:, pairs, 2:4, :], planes[:, pairs, 2:4, :])
 
-        def finish_chunk(c):
-            cols = slice(CHUNK * c, CHUNK * (c + 1))
+        o_bank = [psum.tile([P, N // P, CHUNK], F32, name=f"o_bank{c}") for c in range(CHUNKS)]
+        spare = psum.tile([P, N // P, CHUNK], F32, name="spare", tag="h_bank0")
+
+        def multiply_chunk(c):
             h_codes = keep.tile([P, CHUNK], U32, name=f"h_codes{c}", align_bytes=64)
             h_plane = keep.tile([P, CHUNK], U8, name=f"h_plane{c}", align_bytes=64)
-            nc.vector.quantize_mx(out=h_codes[:].bitcast(FP8X4), scales=h_plane[:], in_=h_bf[c][:])
-            staged = keep.tile([P, N // P, CHUNK], F32, name=f"staged{c}")
+            nc.vector.quantize_mx(
+                out=h_codes[:].bitcast(FP8X4), scales=h_plane[:], in_=h_bf[:, PACK * CHUNK * c : PACK * CHUNK * (c + 1)]
+            )
             for a in range(N // P):
-                o_bank = psum.tile([P, CHUNK], F32, name=f"o_bank{a}", bufs=2)
+                bank = spare if (c, a) == (CHUNKS - 1, 0) else o_bank[c]
                 nc.tensor.matmul_mx(
-                    out=o_bank[:],
+                    out=bank[:, a, :],
                     lhsT=w2_codes[:, 2 * P * a : 2 * P * (a + 1)].bitcast(FP4X4),
                     lhsT_scale=w2_plane[:, P * a : P * (a + 1)],
                     rhs=h_codes[:].bitcast(FP8X4),
@@ -163,14 +162,23 @@ def tile_picked_posadd_none_p_kernel(tc, x_words, x_scales, w1, w2_words, w2_sca
                     start=True,
                     stop=True,
                 )
-                if c == CHUNKS - 1 and a == 0:
-                    nc.vector.tensor_copy(staged[:, a, :], o_bank[:])
-                else:
-                    nc.scalar.copy(staged[:, a, :], o_bank[:])
-            nc.scalar.dma_start(out=out_rows[:, :, cols], in_=staged[:])
 
-        add_chunk(0)
+        def store_chunk(c):
+            staged = keep.tile([P, N // P, CHUNK], F32, name=f"staged{c}")
+            if c == CHUNKS - 1:
+                nc.scalar.copy(staged[:, 0, :], spare[:, 0, :])
+                nc.vector.tensor_copy(staged[:, 1, :], o_bank[c][:, 1, :])
+            elif c == CHUNKS - 2:
+                nc.vector.tensor_copy(staged[:], o_bank[c][:])
+            else:
+                nc.scalar.copy(staged[:], o_bank[c][:])
+            nc.sync.dma_start(out=out_rows[:, :, CHUNK * c : CHUNK * (c + 1)], in_=staged[:])
+
+        for c in range(CHUNKS - 1):
+            sum_last(c)
+        multiply_chunk(0)
+        sum_last(CHUNKS - 1)
         for c in range(1, CHUNKS):
-            add_chunk(c)
-            finish_chunk(c - 1)
-        finish_chunk(CHUNKS - 1)
+            multiply_chunk(c)
+        for c in range(CHUNKS):
+            store_chunk(c)

@@ -20,6 +20,7 @@ PACK = 4
 PASSES = K // (P * PACK)
 HALF = H // 2
 CHUNK = 128
+EARLY_GROUPS = 96
 CHUNKS = S // CHUNK
 
 
@@ -33,7 +34,8 @@ def tile_picked_posadd_none_p_kernel(tc, x_words, x_scales, w1, w2_words, w2_sca
         x_table = [keep.tile([P, T], I32, name=f"x_table{z}") for z in range(PASSES)]
         xs_table = keep.tile([P, T], U8, name="xs_table")
         w1_first = keep.tile([P, PACK, H], F32, name="w1_first")
-        w1_second = [keep.tile([P, PACK, HALF], F32, name=f"w1_second{v}") for v in range(2)]
+        pieces = [slice(0, EARLY_GROUPS), slice(EARLY_GROUPS, P)]
+        w1_second = [keep.tile([P, PACK, PACK * (g.stop - g.start)], F32, name=f"w1_second{g.start}") for g in pieces]
         pe_table = [keep.tile([P, T], F32, name=f"pe_table{t}") for t in range(PACK)]
         w2_codes = keep.tile([P, 2 * N], U8, name="w2_codes", align_bytes=64)
         w2_plane = keep.tile([P, N], U8, name="w2_plane", align_bytes=64)
@@ -54,10 +56,10 @@ def tile_picked_posadd_none_p_kernel(tc, x_words, x_scales, w1, w2_words, w2_sca
                 out=xs_table[32 * q : 32 * q + 4 * PASSES, :].bitcast(I32),
                 in_=x_scales[:, 4 * q : 4 * q + 4, :].bitcast(I32),
             )
-        load_x(1)
         nc.sync.dma_start(out=w1_first[:], in_=w1_rows[0])
-        for v in range(2):
-            nc.sync.dma_start(out=w1_second[v][:], in_=w1_rows[1][:, :, HALF * v : HALF * (v + 1)])
+        load_x(1)
+        for raw, g in zip(w1_second, pieces):
+            nc.sync.dma_start(out=raw[:], in_=w1_rows[1][:, :, PACK * g.start : PACK * g.stop])
         for t in range(PACK):
             nc.sync.dma_start(out=pe_table[t][:], in_=pe_rows[:, t, :])
         nc.sync.dma_start(out=w2_codes[:].bitcast(I32), in_=w2_words[0].bitcast(I32))
@@ -73,17 +75,15 @@ def tile_picked_posadd_none_p_kernel(tc, x_words, x_scales, w1, w2_words, w2_sca
         w1_codes = {zu: keep.tile([P, HALF], U32, name="w1_codes%d%d" % zu, align_bytes=64) for zu in halves}
         w1_plane = {zu: keep.tile([P, HALF], U8, name="w1_plane%d%d" % zu, align_bytes=64) for zu in halves}
         pos_first = keep.tile([P, S], F32, name="pos_first", align_bytes=64)
-        grouped = {zu: keep.tile([P, HALF * PACK], BF16, name="grouped%d%d" % zu, align_bytes=64)[:] for zu in halves[:3]}
-        grouped[1, 1] = pos_first[:].bitcast(BF16)
+        grouped = {zu: keep.tile([P, HALF * PACK], BF16, name="grouped%d%d" % zu, align_bytes=64)[:] for zu in halves}
         h_sum = keep.tile([P, PACK * S], F32, name="h_sum")
         h_bank = [psum.tile([P, S], F32, name=f"h_bank{t}") for t in range(PACK)]
 
-        def round_w1(z, raw, groups):
-            for u, copy in ((1, nc.scalar.copy), (0, nc.vector.tensor_copy)):
-                copy(
-                    grouped[z, u].rearrange("p (t m j) -> p m j t", t=2, j=PACK)[:, groups],
-                    raw[:].rearrange("p j (m t) -> p m j t", t=PACK)[:, :, :, 2 * u : 2 * u + 2],
-                )
+        def round_w1(copy, z, u, raw, first, groups):
+            copy(
+                grouped[z, u].rearrange("p (t m j) -> p m j t", t=2, j=PACK)[:, groups],
+                raw[:].rearrange("p j (m t) -> p m j t", t=PACK)[:, groups.start - first : groups.stop - first, :, 2 * u : 2 * u + 2],
+            )
 
         def pick_x(z):
             nc.vector.tensor_copy(x_codes[z][:], x_table[z][:].bitcast(U32).indirect(offsets[:]))
@@ -92,7 +92,7 @@ def tile_picked_posadd_none_p_kernel(tc, x_words, x_scales, w1, w2_words, w2_sca
             nc.vector.quantize_mx(out=w1_codes[z, u][:].bitcast(FP8X4), scales=w1_plane[z, u][:], in_=grouped[z, u])
 
         def multiply(z, u):
-            for t in (1, 0) if u == 0 else (0, 1):
+            for t in range(2):
                 chans = slice(P * t, P * (t + 1))
                 nc.tensor.matmul_mx(
                     out=h_bank[2 * u + t][:],
@@ -105,23 +105,32 @@ def tile_picked_posadd_none_p_kernel(tc, x_words, x_scales, w1, w2_words, w2_sca
                 )
 
         pick_x(0)
-        pick_x(1)
         nc.vector.tensor_copy(x_planes[:], xs_table[:].indirect(offsets[:]))
-        round_w1(0, w1_first, slice(0, P))
-        for u in range(2):
-            quantize_w1(0, u)
-            multiply(0, u)
-        for v in range(2):
-            round_w1(1, w1_second[v], slice(64 * v, 64 * (v + 1)))
-        for u in range(2):
-            quantize_w1(1, u)
-            multiply(1, u)
-        nc.vector.tensor_copy(pos_first[:], pe_table[0][:].indirect(offsets[:]))
+        round_w1(nc.vector.tensor_copy, 0, 0, w1_first, 0, slice(0, P))
+        round_w1(nc.scalar.copy, 0, 1, w1_first, 0, slice(0, P))
+        quantize_w1(0, 0)
+        multiply(0, 0)
+        pick_x(1)
+        quantize_w1(0, 1)
+        multiply(0, 1)
+        for raw, g in zip(w1_second, pieces):
+            round_w1(nc.scalar.copy, 1, 1, raw, g.start, g)
+            round_w1(nc.vector.tensor_copy, 1, 0, raw, g.start, g)
+        quantize_w1(1, 0)
+        multiply(1, 0)
+        quantize_w1(1, 1)
+        multiply(1, 1)
+        for half in range(2):
+            nc.vector.tensor_copy(
+                pos_first[:, HALF * half : HALF * (half + 1)], pe_table[0][:].indirect(offsets[:, 16 * half : 16 * (half + 1)])
+            )
 
         product = [keep.tile([P, S], F32, name=f"product{t}") for t in range(1, PACK)]
         for t in range(1, PACK):
             nc.scalar.copy(product[t - 1][:], h_bank[t][:])
-        nc.vector.tensor_tensor(h_sum[:, 0:S], h_bank[0][:], pos_first[:], ADD)
+        for half in range(2):
+            cols = slice(HALF * half, HALF * (half + 1))
+            nc.vector.tensor_tensor(h_sum[:, cols], h_bank[0][:, cols], pos_first[:, cols], ADD)
         for t in range(1, PACK - 1):
             nc.vector.tensor_tensor(h_sum[:, S * t : S * (t + 1)], pe_table[t][:].indirect(offsets[:]), product[t - 1][:], ADD)
 

@@ -20,7 +20,7 @@ PACK = 4
 PASSES = K // (P * PACK)
 HALF = H // 2
 CHUNK = 128
-EARLY_GROUPS = 96
+SCALAR_GROUPS = 84
 CHUNKS = S // CHUNK
 
 
@@ -34,8 +34,7 @@ def tile_picked_posadd_none_p_kernel(tc, x_words, x_scales, w1, w2_words, w2_sca
         x_table = [keep.tile([P, T], I32, name=f"x_table{z}") for z in range(PASSES)]
         xs_table = keep.tile([P, T], U8, name="xs_table")
         w1_first = keep.tile([P, PACK, H], F32, name="w1_first")
-        pieces = [slice(0, EARLY_GROUPS), slice(EARLY_GROUPS, P)]
-        w1_second = [keep.tile([P, PACK, PACK * (g.stop - g.start)], F32, name=f"w1_second{g.start}") for g in pieces]
+        w1_second = keep.tile([P, PACK, H], F32, name="w1_second")
         pe_table = [keep.tile([P, T], F32, name=f"pe_table{t}") for t in range(PACK)]
         w2_codes = keep.tile([P, 2 * N], U8, name="w2_codes", align_bytes=64)
         w2_plane = keep.tile([P, N], U8, name="w2_plane", align_bytes=64)
@@ -58,8 +57,7 @@ def tile_picked_posadd_none_p_kernel(tc, x_words, x_scales, w1, w2_words, w2_sca
             )
         nc.sync.dma_start(out=w1_first[:], in_=w1_rows[0])
         load_x(1)
-        for raw, g in zip(w1_second, pieces):
-            nc.sync.dma_start(out=raw[:], in_=w1_rows[1][:, :, PACK * g.start : PACK * g.stop])
+        nc.sync.dma_start(out=w1_second[:], in_=w1_rows[1])
         for t in range(PACK):
             nc.sync.dma_start(out=pe_table[t][:], in_=pe_rows[:, t, :])
         nc.sync.dma_start(out=w2_codes[:].bitcast(I32), in_=w2_words[0].bitcast(I32))
@@ -113,9 +111,9 @@ def tile_picked_posadd_none_p_kernel(tc, x_words, x_scales, w1, w2_words, w2_sca
         pick_x(1)
         quantize_w1(0, 1)
         multiply(0, 1)
-        for raw, g in zip(w1_second, pieces):
-            round_w1(nc.scalar.copy, 1, 1, raw, g.start, g)
-            round_w1(nc.vector.tensor_copy, 1, 0, raw, g.start, g)
+        round_w1(nc.scalar.copy, 1, 1, w1_second, 0, slice(0, SCALAR_GROUPS))
+        round_w1(nc.vector.tensor_copy, 1, 0, w1_second, 0, slice(0, P))
+        round_w1(nc.vector.tensor_copy, 1, 1, w1_second, 0, slice(SCALAR_GROUPS, P))
         quantize_w1(1, 0)
         multiply(1, 0)
         quantize_w1(1, 1)

@@ -170,22 +170,21 @@ def tile_picked_posadd_none_p_kernel(tc, x_words, x_scales, w1, w2_words, w2_sca
                     stop=True,
                 )
 
-        def store_chunk(c):
-            staged = keep.tile([P, N // P, CHUNK], F32, name=f"staged{c}")
-            if c == CHUNKS - 1:
-                nc.scalar.copy(staged[:, 0, :], spare[:, 0, :])
-                nc.vector.tensor_copy(staged[:, 1, :], o_bank[c][:, 1, :])
-            elif c == CHUNKS - 2:
-                nc.vector.tensor_copy(staged[:], o_bank[c][:])
-            else:
-                nc.scalar.copy(staged[:], o_bank[c][:])
-            nc.sync.dma_start(out=out_rows[:, :, CHUNK * c : CHUNK * (c + 1)], in_=staged[:])
-
         for c in range(CHUNKS - 1):
             sum_last(c)
         multiply_chunk(0)
         sum_last(CHUNKS - 1)
         for c in range(1, CHUNKS):
             multiply_chunk(c)
-        for c in range(CHUNKS):
-            store_chunk(c)
+
+        staged_first = h_bf[:, PACK * CHUNK * 2 : PACK * CHUNK * 3].bitcast(F32).rearrange("p (a n) -> p a n", a=N // P)
+        nc.vector.tensor_copy(staged_first, o_bank[0][:])
+        nc.sync.dma_start(out=out_rows[:, :, 0:CHUNK], in_=staged_first)
+        staged_second = keep.tile([P, N // P, CHUNK], F32, name="staged_second")
+        nc.scalar.copy(staged_second[:], o_bank[1][:])
+        nc.sync.dma_start(out=out_rows[:, :, CHUNK : 2 * CHUNK], in_=staged_second[:])
+        staged_rest = keep.tile([P, N // P, 2 * CHUNK], F32, name="staged_rest")
+        nc.scalar.copy(staged_rest[:, :, 0:CHUNK], o_bank[2][:])
+        nc.scalar.copy(staged_rest[:, 0, CHUNK:], spare[:, 0, :])
+        nc.vector.tensor_copy(staged_rest[:, 1, CHUNK:], o_bank[3][:, 1, :])
+        nc.sync.dma_start(out=out_rows[:, :, 2 * CHUNK :], in_=staged_rest[:])

@@ -20,7 +20,7 @@ PACK = 4
 PASSES = K // (P * PACK)
 HALF = H // 2
 CHUNK = 128
-SCALAR_GROUPS = 84
+SCALAR_FIRST = 44
 CHUNKS = S // CHUNK
 
 
@@ -56,8 +56,8 @@ def tile_picked_posadd_none_p_kernel(tc, x_words, x_scales, w1, w2_words, w2_sca
                 in_=x_scales[:, 4 * q : 4 * q + 4, :].bitcast(I32),
             )
         nc.sync.dma_start(out=w1_first[:], in_=w1_rows[0])
-        load_x(1)
         nc.sync.dma_start(out=w1_second[:], in_=w1_rows[1])
+        load_x(1)
         for t in range(PACK):
             nc.sync.dma_start(out=pe_table[t][:], in_=pe_rows[:, t, :])
         nc.sync.dma_start(out=w2_codes[:].bitcast(I32), in_=w2_words[0].bitcast(I32))
@@ -72,10 +72,17 @@ def tile_picked_posadd_none_p_kernel(tc, x_words, x_scales, w1, w2_words, w2_sca
         halves = [(z, u) for z in range(PASSES) for u in range(2)]
         w1_codes = {zu: keep.tile([P, HALF], U32, name="w1_codes%d%d" % zu, align_bytes=64) for zu in halves}
         w1_plane = {zu: keep.tile([P, HALF], U8, name="w1_plane%d%d" % zu, align_bytes=64) for zu in halves}
-        pos_first = keep.tile([P, S], F32, name="pos_first", align_bytes=64)
         grouped = {zu: keep.tile([P, HALF * PACK], BF16, name="grouped%d%d" % zu, align_bytes=64)[:] for zu in halves}
         h_sum = keep.tile([P, PACK * S], F32, name="h_sum")
-        h_bank = [psum.tile([P, S], F32, name=f"h_bank{t}") for t in range(PACK)]
+        whole = slice(0, S)
+        list_halves = [slice(0, S // 2), slice(S // 2, S)]
+        x_pieces = [slice(0, S // 4), slice(S // 4, S // 2), slice(S // 2, S)]
+        pieces = {0: x_pieces, 1: list_halves, 2: [whole], 3: [whole]}
+        h_bank = {
+            (t, cols.start): psum.tile([P, cols.stop - cols.start], F32, name=f"h_bank{t}_{cols.start}")
+            for t in range(PACK)
+            for cols in pieces[t]
+        }
 
         def round_w1(copy, z, u, raw, first, groups):
             copy(
@@ -83,54 +90,65 @@ def tile_picked_posadd_none_p_kernel(tc, x_words, x_scales, w1, w2_words, w2_sca
                 raw[:].rearrange("p j (m t) -> p m j t", t=PACK)[:, groups.start - first : groups.stop - first, :, 2 * u : 2 * u + 2],
             )
 
-        def pick_x(z):
-            nc.vector.tensor_copy(x_codes[z][:], x_table[z][:].bitcast(U32).indirect(offsets[:]))
+        def entries(cols):
+            return offsets[:, cols.start // 16 : cols.stop // 16]
+
+        def pick_x(z, cols):
+            nc.vector.tensor_copy(x_codes[z][:, cols], x_table[z][:].bitcast(U32).indirect(entries(cols)))
 
         def quantize_w1(z, u):
             nc.vector.quantize_mx(out=w1_codes[z, u][:].bitcast(FP8X4), scales=w1_plane[z, u][:], in_=grouped[z, u])
 
-        def multiply(z, u):
-            for t in range(2):
-                chans = slice(P * t, P * (t + 1))
-                nc.tensor.matmul_mx(
-                    out=h_bank[2 * u + t][:],
-                    lhsT=w1_codes[z, u][:, chans].bitcast(FP8X4),
-                    lhsT_scale=w1_plane[z, u][:, chans],
-                    rhs=x_codes[z][:].bitcast(FP8X4),
-                    rhs_scale=x_planes[4 * z :, :],
-                    start=(z == 0),
-                    stop=(z == PASSES - 1),
-                )
+        def multiply(z, t, cols):
+            u = t // 2
+            chans = slice(P * (t % 2), P * (t % 2 + 1))
+            nc.tensor.matmul_mx(
+                out=h_bank[t, cols.start][:],
+                lhsT=w1_codes[z, u][:, chans].bitcast(FP8X4),
+                lhsT_scale=w1_plane[z, u][:, chans],
+                rhs=x_codes[z][:, cols].bitcast(FP8X4),
+                rhs_scale=x_planes[4 * z :, cols],
+                start=(z == 0),
+                stop=(z == PASSES - 1),
+            )
 
-        pick_x(0)
+        pick_x(0, whole)
         nc.vector.tensor_copy(x_planes[:], xs_table[:].indirect(offsets[:]))
         round_w1(nc.vector.tensor_copy, 0, 0, w1_first, 0, slice(0, P))
         round_w1(nc.scalar.copy, 0, 1, w1_first, 0, slice(0, P))
-        quantize_w1(0, 0)
-        multiply(0, 0)
-        pick_x(1)
-        quantize_w1(0, 1)
-        multiply(0, 1)
-        round_w1(nc.scalar.copy, 1, 1, w1_second, 0, slice(0, SCALAR_GROUPS))
-        round_w1(nc.vector.tensor_copy, 1, 0, w1_second, 0, slice(0, P))
-        round_w1(nc.vector.tensor_copy, 1, 1, w1_second, 0, slice(SCALAR_GROUPS, P))
+        for u in range(2):
+            quantize_w1(0, u)
+            for t in (2 * u, 2 * u + 1):
+                for cols in pieces[t]:
+                    multiply(0, t, cols)
+        round_w1(nc.scalar.copy, 1, 0, w1_second, 0, slice(0, SCALAR_FIRST))
+        round_w1(nc.vector.tensor_copy, 1, 0, w1_second, 0, slice(SCALAR_FIRST, P))
+        round_w1(nc.scalar.copy, 1, 1, w1_second, 0, slice(0, P))
         quantize_w1(1, 0)
-        multiply(1, 0)
+        product = [keep.tile([P, S], F32, name=f"product{t}") for t in range(PACK)]
+
+        def finish_product(t, cols):
+            multiply(1, t, cols)
+            nc.scalar.copy(product[t][:, cols], h_bank[t, cols.start][:])
+
+        for cols in x_pieces:
+            pick_x(1, cols)
+            finish_product(0, cols)
+            if cols.stop % (S // 2) == 0:
+                finish_product(1, slice(cols.stop - S // 2, cols.stop))
         quantize_w1(1, 1)
-        multiply(1, 1)
-        for half in range(2):
-            nc.vector.tensor_copy(
-                pos_first[:, HALF * half : HALF * (half + 1)], pe_table[0][:].indirect(offsets[:, 16 * half : 16 * (half + 1)])
+        for t in (2, 3):
+            finish_product(t, whole)
+
+        def add_position(t, cols):
+            nc.vector.tensor_tensor(
+                h_sum[:, S * t + cols.start : S * t + cols.stop], pe_table[t][:].indirect(entries(cols)), product[t][:, cols], ADD
             )
 
-        product = [keep.tile([P, S], F32, name=f"product{t}") for t in range(1, PACK)]
-        for t in range(1, PACK):
-            nc.scalar.copy(product[t - 1][:], h_bank[t][:])
-        for half in range(2):
-            cols = slice(HALF * half, HALF * (half + 1))
-            nc.vector.tensor_tensor(h_sum[:, cols], h_bank[0][:, cols], pos_first[:, cols], ADD)
+        for cols in x_pieces:
+            add_position(0, cols)
         for t in range(1, PACK - 1):
-            nc.vector.tensor_tensor(h_sum[:, S * t : S * (t + 1)], pe_table[t][:].indirect(offsets[:]), product[t - 1][:], ADD)
+            add_position(t, whole)
 
         h_bf = keep.tile([P, S * PACK], BF16, name="h_bf", align_bytes=64)
         woven = h_bf[:].rearrange("p (b i t) -> p b t i", i=2, t=PACK)
@@ -138,19 +156,19 @@ def tile_picked_posadd_none_p_kernel(tc, x_words, x_scales, w1, w2_words, w2_sca
         nc.scalar.copy(woven[:, :, 0:2, :], planes[:, :, 0:2, :])
         out_rows = out.rearrange("(a p) n -> p a n", p=P)
 
+        def weave_last(copy, cols):
+            pairs = slice(cols.start // 2, cols.stop // 2)
+            copy(woven[:, pairs, 2:4, :], planes[:, pairs, 2:4, :])
+
         def sum_last(c):
             cols = slice(CHUNK * c, CHUNK * (c + 1))
-            nc.vector.tensor_tensor(
-                h_sum[:, 3 * S + CHUNK * c : 3 * S + CHUNK * (c + 1)],
-                pe_table[3][:].indirect(offsets[:, CHUNK * c // 16 : CHUNK * (c + 1) // 16]),
-                product[2][:, cols],
-                ADD,
-            )
-            pairs = slice(CHUNK * c // 2, CHUNK * (c + 1) // 2)
-            nc.scalar.copy(woven[:, pairs, 2:4, :], planes[:, pairs, 2:4, :])
+            add_position(3, cols)
+            stop = cols.stop - CHUNK // 2 if c == 1 else cols.stop
+            weave_last(nc.scalar.copy, slice(cols.start, stop))
 
-        o_bank = [psum.tile([P, N // P, CHUNK], F32, name=f"o_bank{c}") for c in range(CHUNKS)]
-        spare = psum.tile([P, N // P, CHUNK], F32, name="spare", tag="h_bank0")
+        o_tags = ["o_bank", "h_bank0_0", "h_bank0_128", "h_bank0_256"]
+        o_bank = [psum.tile([P, N // P, CHUNK], F32, name=f"o_bank{c}", tag=o_tags[c]) for c in range(CHUNKS)]
+        spare = psum.tile([P, N // P, CHUNK], F32, name="spare", tag="h_bank1_0")
 
         def multiply_chunk(c):
             h_codes = keep.tile([P, CHUNK], U32, name=f"h_codes{c}", align_bytes=64)
@@ -170,19 +188,18 @@ def tile_picked_posadd_none_p_kernel(tc, x_words, x_scales, w1, w2_words, w2_sca
                     stop=True,
                 )
 
-        for c in range(CHUNKS - 1):
+        for c in range(CHUNKS):
             sum_last(c)
-        multiply_chunk(0)
-        sum_last(CHUNKS - 1)
-        for c in range(1, CHUNKS):
+        weave_last(nc.vector.tensor_copy, slice(2 * CHUNK - CHUNK // 2, 2 * CHUNK))
+        for c in range(CHUNKS):
             multiply_chunk(c)
 
-        staged_first = h_bf[:, PACK * CHUNK * 2 : PACK * CHUNK * 3].bitcast(F32).rearrange("p (a n) -> p a n", a=N // P)
-        nc.vector.tensor_copy(staged_first, o_bank[0][:])
-        nc.sync.dma_start(out=out_rows[:, :, 0:CHUNK], in_=staged_first)
-        staged_second = keep.tile([P, N // P, CHUNK], F32, name="staged_second")
-        nc.scalar.copy(staged_second[:], o_bank[1][:])
-        nc.sync.dma_start(out=out_rows[:, :, CHUNK : 2 * CHUNK], in_=staged_second[:])
+        staged_first = keep.tile([P, N // P, CHUNK], F32, name="staged_first")
+        nc.scalar.copy(staged_first[:], o_bank[0][:])
+        nc.sync.dma_start(out=out_rows[:, :, 0:CHUNK], in_=staged_first[:])
+        staged_second = h_bf[:, PACK * CHUNK * 3 :].bitcast(F32).rearrange("p (a n) -> p a n", a=N // P)
+        nc.vector.tensor_copy(staged_second, o_bank[1][:])
+        nc.sync.dma_start(out=out_rows[:, :, CHUNK : 2 * CHUNK], in_=staged_second)
         staged_rest = keep.tile([P, N // P, 2 * CHUNK], F32, name="staged_rest")
         nc.scalar.copy(staged_rest[:, :, 0:CHUNK], o_bank[2][:])
         nc.scalar.copy(staged_rest[:, 0, CHUNK:], spare[:, 0, :])

@@ -80,7 +80,7 @@ def tile_picked_posadd_none_p_kernel(tc, x_words, x_scales, w1, w2_words, w2_sca
         pieces = {0: x_pieces, 1: list_halves, 2: [whole], 3: [whole]}
         h_bank = {
             (t, cols.start): psum.tile([P, cols.stop - cols.start], F32, name=f"h_bank{t}_{cols.start}")
-            for t in range(PACK)
+            for t in range(PACK - 1)
             for cols in pieces[t]
         }
 
@@ -118,14 +118,17 @@ def tile_picked_posadd_none_p_kernel(tc, x_words, x_scales, w1, w2_words, w2_sca
         round_w1(nc.scalar.copy, 0, 1, w1_first, 0, slice(0, P))
         for u in range(2):
             quantize_w1(0, u)
-            for t in (2 * u, 2 * u + 1):
+            for t in range(2 * u, min(2 * u + 2, PACK - 1)):
                 for cols in pieces[t]:
                     multiply(0, t, cols)
         round_w1(nc.scalar.copy, 1, 0, w1_second, 0, slice(0, SCALAR_FIRST))
         round_w1(nc.vector.tensor_copy, 1, 0, w1_second, 0, slice(SCALAR_FIRST, P))
         round_w1(nc.scalar.copy, 1, 1, w1_second, 0, slice(0, P))
         quantize_w1(1, 0)
-        product = [keep.tile([P, S], F32, name=f"product{t}") for t in range(PACK)]
+        product = {t: keep.tile([P, S], F32, name=f"product{t}")[:] for t in (1, 3)}
+        shared = keep.tile([P, S + S // 2], F32, name="shared")
+        product[0] = shared[:, S // 2 :]
+        product[2] = shared[:, 0:S]
 
         def finish_product(t, cols):
             multiply(1, t, cols)
@@ -137,34 +140,53 @@ def tile_picked_posadd_none_p_kernel(tc, x_words, x_scales, w1, w2_words, w2_sca
             if cols.stop % (S // 2) == 0:
                 finish_product(1, slice(cols.stop - S // 2, cols.stop))
         quantize_w1(1, 1)
-        for t in (2, 3):
-            finish_product(t, whole)
+        multiply(1, 2, whole)
 
         def add_position(t, cols):
-            nc.vector.tensor_tensor(
-                h_sum[:, S * t + cols.start : S * t + cols.stop], pe_table[t][:].indirect(entries(cols)), product[t][:, cols], ADD
-            )
+            if t == PACK - 1 and cols.start >= S // 2:
+                sums = shared[:, cols.start - S // 2 : cols.stop - S // 2]
+            else:
+                sums = product[t][:, cols]
+            nc.vector.tensor_tensor(h_sum[:, S * t + cols.start : S * t + cols.stop], pe_table[t][:].indirect(entries(cols)), sums, ADD)
 
         for cols in x_pieces:
             add_position(0, cols)
+        nc.scalar.copy(product[2], h_bank[2, 0][:])
+        h_bank[3, 0] = psum.tile([P, S], F32, name="h_bank3_0", tag="h_bank2_0")
+        for z in range(PASSES):
+            multiply(z, 3, whole)
+        nc.scalar.copy(product[3][:, 0 : S // 2], h_bank[3, 0][:, 0 : S // 2])
         for t in range(1, PACK - 1):
             add_position(t, whole)
+        late = shared[:, 0 : S // 2]
+        nc.scalar.copy(late, h_bank[3, 0][:, S // 2 :])
+        unread = psum.tile([P, S], F32, name="unread", tag="h_bank2_0")
+        for z in range(PASSES):
+            nc.tensor.matmul_mx(
+                out=unread[:],
+                lhsT=w1_codes[z, 0][:, 0:P].bitcast(FP8X4),
+                lhsT_scale=w1_plane[z, 0][:, 0:P],
+                rhs=x_codes[z][:].bitcast(FP8X4),
+                rhs_scale=x_planes[4 * z :, :],
+                start=(z == 0),
+                stop=(z == PASSES - 1),
+            )
 
         h_bf = keep.tile([P, S * PACK], BF16, name="h_bf", align_bytes=64)
-        woven = h_bf[:].rearrange("p (b i t) -> p b t i", i=2, t=PACK)
-        planes = h_sum[:].rearrange("p (t b i) -> p b t i", i=2, t=PACK)
-        nc.scalar.copy(woven[:, :, 0:2, :], planes[:, :, 0:2, :])
+        woven = h_bf[:].rearrange("p (b i t) -> p b t i", i=4, t=PACK)
+        planes = h_sum[:].rearrange("p (t b i) -> p b t i", i=4, t=PACK)
         out_rows = out.rearrange("(a p) n -> p a n", p=P)
 
         def weave_last(copy, cols):
-            pairs = slice(cols.start // 2, cols.stop // 2)
-            copy(woven[:, pairs, 2:4, :], planes[:, pairs, 2:4, :])
+            quads = slice(cols.start // 4, cols.stop // 4)
+            copy(woven[:, quads], planes[:, quads])
 
         def sum_last(c):
             cols = slice(CHUNK * c, CHUNK * (c + 1))
             add_position(3, cols)
+            start = cols.start + CHUNK // 2 if c == 2 else cols.start
             stop = cols.stop - CHUNK // 2 if c == 1 else cols.stop
-            weave_last(nc.scalar.copy, slice(cols.start, stop))
+            weave_last(nc.scalar.copy, slice(start, stop))
 
         o_tags = ["o_bank", "h_bank0_0", "h_bank0_128", "h_bank0_256"]
         o_bank = [psum.tile([P, N // P, CHUNK], F32, name=f"o_bank{c}", tag=o_tags[c]) for c in range(CHUNKS)]
@@ -190,7 +212,7 @@ def tile_picked_posadd_none_p_kernel(tc, x_words, x_scales, w1, w2_words, w2_sca
 
         for c in range(CHUNKS):
             sum_last(c)
-        weave_last(nc.vector.tensor_copy, slice(2 * CHUNK - CHUNK // 2, 2 * CHUNK))
+        weave_last(nc.vector.tensor_copy, slice(2 * CHUNK - CHUNK // 2, 2 * CHUNK + CHUNK // 2))
         for c in range(CHUNKS):
             multiply_chunk(c)
 

@@ -143,23 +143,19 @@ def tile_picked_posadd_none_p_kernel(tc, x_words, x_scales, w1, w2_words, w2_sca
         multiply(1, 2, whole)
 
         def add_position(t, cols):
-            if t == PACK - 1 and cols.start >= S // 2:
-                sums = shared[:, cols.start - S // 2 : cols.stop - S // 2]
-            else:
-                sums = product[t][:, cols]
-            nc.vector.tensor_tensor(h_sum[:, S * t + cols.start : S * t + cols.stop], pe_table[t][:].indirect(entries(cols)), sums, ADD)
+            nc.vector.tensor_tensor(
+                h_sum[:, S * t + cols.start : S * t + cols.stop], pe_table[t][:].indirect(entries(cols)), product[t][:, cols], ADD
+            )
 
         for cols in x_pieces:
             add_position(0, cols)
         nc.scalar.copy(product[2], h_bank[2, 0][:])
-        h_bank[3, 0] = psum.tile([P, S], F32, name="h_bank3_0", tag="h_bank2_0")
-        for z in range(PASSES):
-            multiply(z, 3, whole)
-        nc.scalar.copy(product[3][:, 0 : S // 2], h_bank[3, 0][:, 0 : S // 2])
+        for cols in list_halves:
+            h_bank[3, cols.start] = psum.tile([P, S // 2], F32, name=f"h_bank3_{cols.start}", tag="h_bank2_0")
+            multiply(0, 3, cols)
+            finish_product(3, cols)
         for t in range(1, PACK - 1):
             add_position(t, whole)
-        late = shared[:, 0 : S // 2]
-        nc.scalar.copy(late, h_bank[3, 0][:, S // 2 :])
         unread = psum.tile([P, S], F32, name="unread", tag="h_bank2_0")
         for z in range(PASSES):
             nc.tensor.matmul_mx(
@@ -177,16 +173,19 @@ def tile_picked_posadd_none_p_kernel(tc, x_words, x_scales, w1, w2_words, w2_sca
         planes = h_sum[:].rearrange("p (t b i) -> p b t i", i=4, t=PACK)
         out_rows = out.rearrange("(a p) n -> p a n", p=P)
 
-        def weave_last(copy, cols):
+        def weave(copy, cols, rows):
             quads = slice(cols.start // 4, cols.stop // 4)
-            copy(woven[:, quads], planes[:, quads])
+            copy(woven[:, quads, rows], planes[:, quads, rows])
+
+        for c in (0, CHUNKS - 1):
+            weave(nc.scalar.copy, slice(CHUNK * c, CHUNK * (c + 1)), slice(0, 2))
 
         def sum_last(c):
             cols = slice(CHUNK * c, CHUNK * (c + 1))
             add_position(3, cols)
-            start = cols.start + CHUNK // 2 if c == 2 else cols.start
-            stop = cols.stop - CHUNK // 2 if c == 1 else cols.stop
-            weave_last(nc.scalar.copy, slice(start, stop))
+            start = cols.start + CHUNK // 4 if c == 2 else cols.start
+            stop = cols.stop - CHUNK // 4 if c == 1 else cols.stop
+            weave(nc.scalar.copy, slice(start, stop), slice(2 if c in (0, CHUNKS - 1) else 0, PACK))
 
         o_tags = ["o_bank", "h_bank0_0", "h_bank0_128", "h_bank0_256"]
         o_bank = [psum.tile([P, N // P, CHUNK], F32, name=f"o_bank{c}", tag=o_tags[c]) for c in range(CHUNKS)]
@@ -212,7 +211,7 @@ def tile_picked_posadd_none_p_kernel(tc, x_words, x_scales, w1, w2_words, w2_sca
 
         for c in range(CHUNKS):
             sum_last(c)
-        weave_last(nc.vector.tensor_copy, slice(2 * CHUNK - CHUNK // 2, 2 * CHUNK + CHUNK // 2))
+        weave(nc.vector.tensor_copy, slice(2 * CHUNK - CHUNK // 4, 2 * CHUNK + CHUNK // 4), slice(0, PACK))
         for c in range(CHUNKS):
             multiply_chunk(c)
 

@@ -14,13 +14,13 @@ U8 = mybir.dt.uint8
 FP8X4 = mybir.dt.float8_e4m3fn_x4
 FP4X4 = mybir.dt.float4_e2m1fn_x4
 ADD = mybir.AluOpType.add
+COPY = mybir.ActivationFunctionType.Copy
 
 P = 128
 PACK = 4
 PASSES = K // (P * PACK)
 HALF = H // 2
 CHUNK = 128
-SCALAR_FIRST = 44
 CHUNKS = S // CHUNK
 
 
@@ -69,25 +69,20 @@ def tile_picked_posadd_none_p_kernel(tc, x_words, x_scales, w1, w2_words, w2_sca
 
         x_codes = [keep.tile([P, S], U32, name=f"x_codes{z}", align_bytes=64) for z in range(PASSES)]
         x_planes = keep.tile([P, S], U8, name="x_planes", align_bytes=64)
-        halves = [(z, u) for z in range(PASSES) for u in range(2)]
-        w1_codes = {zu: keep.tile([P, HALF], U32, name="w1_codes%d%d" % zu, align_bytes=64) for zu in halves}
-        w1_plane = {zu: keep.tile([P, HALF], U8, name="w1_plane%d%d" % zu, align_bytes=64) for zu in halves}
-        grouped = {zu: keep.tile([P, HALF * PACK], BF16, name="grouped%d%d" % zu, align_bytes=64)[:] for zu in halves}
-        h_sum = keep.tile([P, PACK * S], F32, name="h_sum")
+        pairs = [(z, u) for z in range(PASSES) for u in range(2)]
+        w1_codes = {zu: keep.tile([P, HALF], U32, name="w1_codes%d%d" % zu, align_bytes=64) for zu in pairs}
+        w1_plane = {zu: keep.tile([P, HALF], U8, name="w1_plane%d%d" % zu, align_bytes=64) for zu in pairs}
+        grouped = {zu: keep.tile([P, HALF * PACK], BF16, name="grouped%d%d" % zu, align_bytes=64)[:] for zu in pairs}
+        pe_picked = [keep.tile([P, 2, S], F32, name=f"pe_picked{u}") for u in range(2)]
+        h_bf = keep.tile([P, S, PACK], BF16, name="h_bf", align_bytes=64)
         whole = slice(0, S)
         list_halves = [slice(0, S // 2), slice(S // 2, S)]
-        x_pieces = [slice(0, S // 4), slice(S // 4, S // 2), slice(S // 2, S)]
-        pieces = {0: x_pieces, 1: list_halves, 2: [whole], 3: [whole]}
-        h_bank = {
-            (t, cols.start): psum.tile([P, cols.stop - cols.start], F32, name=f"h_bank{t}_{cols.start}")
-            for t in range(PACK - 1)
-            for cols in pieces[t]
-        }
+        h_bank = {(u, v): psum.tile([P, 2, S // 2], F32, name=f"h_bank{u}{v}") for u in range(2) for v in range(2)}
 
-        def round_w1(copy, z, u, raw, first, groups):
+        def round_w1(copy, z, u, raw):
             copy(
-                grouped[z, u].rearrange("p (t m j) -> p m j t", t=2, j=PACK)[:, groups],
-                raw[:].rearrange("p j (m t) -> p m j t", t=PACK)[:, groups.start - first : groups.stop - first, :, 2 * u : 2 * u + 2],
+                grouped[z, u].rearrange("p (t m j) -> p m j t", t=2, j=PACK),
+                raw[:].rearrange("p j (m t) -> p m j t", t=PACK)[:, :, :, 2 * u : 2 * u + 2],
             )
 
         def entries(cols):
@@ -99,108 +94,77 @@ def tile_picked_posadd_none_p_kernel(tc, x_words, x_scales, w1, w2_words, w2_sca
         def quantize_w1(z, u):
             nc.vector.quantize_mx(out=w1_codes[z, u][:].bitcast(FP8X4), scales=w1_plane[z, u][:], in_=grouped[z, u])
 
-        def multiply(z, t, cols):
-            u = t // 2
-            chans = slice(P * (t % 2), P * (t % 2 + 1))
-            nc.tensor.matmul_mx(
-                out=h_bank[t, cols.start][:],
-                lhsT=w1_codes[z, u][:, chans].bitcast(FP8X4),
-                lhsT_scale=w1_plane[z, u][:, chans],
-                rhs=x_codes[z][:, cols].bitcast(FP8X4),
-                rhs_scale=x_planes[4 * z :, cols],
-                start=(z == 0),
-                stop=(z == PASSES - 1),
+        def multiply(z, u, v):
+            cols = list_halves[v]
+            for e in range(2):
+                chans = slice(P * e, P * (e + 1))
+                nc.tensor.matmul_mx(
+                    out=h_bank[u, v][:, e, :],
+                    lhsT=w1_codes[z, u][:, chans].bitcast(FP8X4),
+                    lhsT_scale=w1_plane[z, u][:, chans],
+                    rhs=x_codes[z][:, cols].bitcast(FP8X4),
+                    rhs_scale=x_planes[4 * z :, cols],
+                    start=(z == 0 and e == 0),
+                    stop=(z == PASSES - 1 and e == 1),
+                )
+
+        def pick_pe(engine, t, cols):
+            picked = pe_picked[t // 2][:, t % 2, cols]
+            window = pe_table[t][:].indirect(entries(cols))
+            if engine is nc.scalar:
+                nc.scalar.activation(picked, window, COPY)
+            else:
+                nc.vector.tensor_copy(picked, window)
+
+        def add_pair(u, cols):
+            v = cols.start // (S // 2)
+            in_bank = slice(cols.start - v * S // 2, cols.stop - v * S // 2)
+            nc.vector.tensor_tensor(
+                h_bf[:, cols, 2 * u : 2 * u + 2],
+                h_bank[u, v][:, :, in_bank].rearrange("p e c -> p c e"),
+                pe_picked[u][:, :, cols].rearrange("p e c -> p c e"),
+                ADD,
             )
 
         pick_x(0, whole)
         nc.vector.tensor_copy(x_planes[:], xs_table[:].indirect(offsets[:]))
-        round_w1(nc.vector.tensor_copy, 0, 0, w1_first, 0, slice(0, P))
-        round_w1(nc.scalar.copy, 0, 1, w1_first, 0, slice(0, P))
-        for u in range(2):
-            quantize_w1(0, u)
-            for t in range(2 * u, min(2 * u + 2, PACK - 1)):
-                for cols in pieces[t]:
-                    multiply(0, t, cols)
-        round_w1(nc.scalar.copy, 1, 0, w1_second, 0, slice(0, SCALAR_FIRST))
-        round_w1(nc.vector.tensor_copy, 1, 0, w1_second, 0, slice(SCALAR_FIRST, P))
-        round_w1(nc.scalar.copy, 1, 1, w1_second, 0, slice(0, P))
+        for z, raw in enumerate((w1_first, w1_second)):
+            round_w1(nc.vector.tensor_copy, z, 0, raw)
+            round_w1(nc.scalar.copy, z, 1, raw)
+            if z == 0:
+                for u in range(2):
+                    quantize_w1(0, u)
+                    for v in range(2):
+                        multiply(0, u, v)
         quantize_w1(1, 0)
-        product = {t: keep.tile([P, S], F32, name=f"product{t}")[:] for t in (1, 3)}
-        shared = keep.tile([P, S + S // 2], F32, name="shared")
-        product[0] = shared[:, S // 2 :]
-        product[2] = shared[:, 0:S]
-
-        def finish_product(t, cols):
-            multiply(1, t, cols)
-            nc.scalar.copy(product[t][:, cols], h_bank[t, cols.start][:])
-
-        for cols in x_pieces:
-            pick_x(1, cols)
-            finish_product(0, cols)
-            if cols.stop % (S // 2) == 0:
-                finish_product(1, slice(cols.stop - S // 2, cols.stop))
+        for v in range(2):
+            pick_x(1, list_halves[v])
+            multiply(1, 0, v)
         quantize_w1(1, 1)
-        multiply(1, 2, whole)
+        for v in range(2):
+            multiply(1, 1, v)
 
-        def add_position(t, cols):
-            nc.vector.tensor_tensor(
-                h_sum[:, S * t + cols.start : S * t + cols.stop], pe_table[t][:].indirect(entries(cols)), product[t][:, cols], ADD
-            )
-
-        for cols in x_pieces:
-            add_position(0, cols)
-        nc.scalar.copy(product[2], h_bank[2, 0][:])
+        pick_pe(nc.scalar, 0, whole)
+        pick_pe(nc.vector, 1, list_halves[0])
+        pick_pe(nc.scalar, 1, list_halves[1])
         for cols in list_halves:
-            h_bank[3, cols.start] = psum.tile([P, S // 2], F32, name=f"h_bank3_{cols.start}", tag="h_bank2_0")
-            multiply(0, 3, cols)
-            finish_product(3, cols)
-        for t in range(1, PACK - 1):
-            add_position(t, whole)
-        unread = psum.tile([P, S], F32, name="unread", tag="h_bank2_0")
-        for z in range(PASSES):
-            nc.tensor.matmul_mx(
-                out=unread[:],
-                lhsT=w1_codes[z, 0][:, 0:P].bitcast(FP8X4),
-                lhsT_scale=w1_plane[z, 0][:, 0:P],
-                rhs=x_codes[z][:].bitcast(FP8X4),
-                rhs_scale=x_planes[4 * z :, :],
-                start=(z == 0),
-                stop=(z == PASSES - 1),
-            )
+            add_pair(0, cols)
+        pick_pe(nc.scalar, 2, whole)
 
-        h_bf = keep.tile([P, S * PACK], BF16, name="h_bf", align_bytes=64)
-        woven = h_bf[:].rearrange("p (b i t) -> p b t i", i=4, t=PACK)
-        planes = h_sum[:].rearrange("p (t b i) -> p b t i", i=4, t=PACK)
         out_rows = out.rearrange("(a p) n -> p a n", p=P)
-
-        def weave(copy, cols, rows):
-            quads = slice(cols.start // 4, cols.stop // 4)
-            copy(woven[:, quads, rows], planes[:, quads, rows])
-
-        for c in (0, CHUNKS - 1):
-            weave(nc.scalar.copy, slice(CHUNK * c, CHUNK * (c + 1)), slice(0, 2))
-
-        def sum_last(c):
-            cols = slice(CHUNK * c, CHUNK * (c + 1))
-            add_position(3, cols)
-            start = cols.start + CHUNK // 4 if c == 2 else cols.start
-            stop = cols.stop - CHUNK // 4 if c == 1 else cols.stop
-            weave(nc.scalar.copy, slice(start, stop), slice(2 if c in (0, CHUNKS - 1) else 0, PACK))
-
-        o_tags = ["o_bank", "h_bank0_0", "h_bank0_128", "h_bank0_256"]
-        o_bank = [psum.tile([P, N // P, CHUNK], F32, name=f"o_bank{c}", tag=o_tags[c]) for c in range(CHUNKS)]
-        spare = psum.tile([P, N // P, CHUNK], F32, name="spare", tag="h_bank1_0")
+        chunks = [slice(CHUNK * c, CHUNK * (c + 1)) for c in range(CHUNKS)]
+        o_bank = [psum.tile([P, N // P, CHUNK], F32, name=f"o_bank{c}") for c in range(CHUNKS)]
+        spare = psum.tile([P, CHUNK], F32, name="spare", tag="h_bank00")
 
         def multiply_chunk(c):
             h_codes = keep.tile([P, CHUNK], U32, name=f"h_codes{c}", align_bytes=64)
             h_plane = keep.tile([P, CHUNK], U8, name=f"h_plane{c}", align_bytes=64)
             nc.vector.quantize_mx(
-                out=h_codes[:].bitcast(FP8X4), scales=h_plane[:], in_=h_bf[:, PACK * CHUNK * c : PACK * CHUNK * (c + 1)]
+                out=h_codes[:].bitcast(FP8X4), scales=h_plane[:], in_=h_bf[:, chunks[c], :].rearrange("p c t -> p (c t)")
             )
             for a in range(N // P):
-                bank = spare if (c, a) == (CHUNKS - 1, 0) else o_bank[c]
                 nc.tensor.matmul_mx(
-                    out=bank[:, a, :],
+                    out=spare[:] if (c, a) == (CHUNKS - 1, 0) else o_bank[c][:, a, :],
                     lhsT=w2_codes[:, 2 * P * a : 2 * P * (a + 1)].bitcast(FP4X4),
                     lhsT_scale=w2_plane[:, P * a : P * (a + 1)],
                     rhs=h_codes[:].bitcast(FP8X4),
@@ -210,19 +174,19 @@ def tile_picked_posadd_none_p_kernel(tc, x_words, x_scales, w1, w2_words, w2_sca
                 )
 
         for c in range(CHUNKS):
-            sum_last(c)
-        weave(nc.vector.tensor_copy, slice(2 * CHUNK - CHUNK // 4, 2 * CHUNK + CHUNK // 4), slice(0, PACK))
+            pick_pe(nc.scalar, 3, chunks[c])
         for c in range(CHUNKS):
-            multiply_chunk(c)
+            add_pair(1, chunks[c])
+            if c > 0:
+                multiply_chunk(c - 1)
+        multiply_chunk(CHUNKS - 1)
 
-        staged_first = keep.tile([P, N // P, CHUNK], F32, name="staged_first")
-        nc.scalar.copy(staged_first[:], o_bank[0][:])
-        nc.sync.dma_start(out=out_rows[:, :, 0:CHUNK], in_=staged_first[:])
-        staged_second = h_bf[:, PACK * CHUNK * 3 :].bitcast(F32).rearrange("p (a n) -> p a n", a=N // P)
-        nc.vector.tensor_copy(staged_second, o_bank[1][:])
-        nc.sync.dma_start(out=out_rows[:, :, CHUNK : 2 * CHUNK], in_=staged_second)
-        staged_rest = keep.tile([P, N // P, 2 * CHUNK], F32, name="staged_rest")
-        nc.scalar.copy(staged_rest[:, :, 0:CHUNK], o_bank[2][:])
-        nc.scalar.copy(staged_rest[:, 0, CHUNK:], spare[:, 0, :])
-        nc.vector.tensor_copy(staged_rest[:, 1, CHUNK:], o_bank[3][:, 1, :])
-        nc.sync.dma_start(out=out_rows[:, :, 2 * CHUNK :], in_=staged_rest[:])
+        staged = keep.tile([P, N // P, S], F32, name="staged")
+        for c in range(CHUNKS - 1):
+            nc.scalar.copy(staged[:, :, chunks[c]], o_bank[c][:])
+            if c > 0:
+                cols = slice(0, 2 * CHUNK) if c == 1 else chunks[c]
+                nc.sync.dma_start(out=out_rows[:, :, cols], in_=staged[:, :, cols])
+        nc.scalar.copy(staged[:, 0, chunks[-1]], spare[:])
+        nc.vector.tensor_copy(staged[:, 1, chunks[-1]], o_bank[-1][:, 1, :])
+        nc.sync.dma_start(out=out_rows[:, :, chunks[-1]], in_=staged[:, :, chunks[-1]])

@@ -55,9 +55,9 @@ def tile_picked_posadd_none_p_kernel(tc, x_words, x_scales, w1, w2_words, w2_sca
                 out=xs_table[32 * q : 32 * q + 4 * PASSES, :].bitcast(I32),
                 in_=x_scales[:, 4 * q : 4 * q + 4, :].bitcast(I32),
             )
+        load_x(1)
         nc.sync.dma_start(out=w1_first[:], in_=w1_rows[0])
         nc.sync.dma_start(out=w1_second[:], in_=w1_rows[1])
-        load_x(1)
         for t in range(PACK):
             nc.sync.dma_start(out=pe_table[t][:], in_=pe_rows[:, t, :])
         nc.sync.dma_start(out=w2_codes[:].bitcast(I32), in_=w2_words[0].bitcast(I32))
@@ -73,11 +73,13 @@ def tile_picked_posadd_none_p_kernel(tc, x_words, x_scales, w1, w2_words, w2_sca
         w1_codes = {zu: keep.tile([P, HALF], U32, name="w1_codes%d%d" % zu, align_bytes=64) for zu in pairs}
         w1_plane = {zu: keep.tile([P, HALF], U8, name="w1_plane%d%d" % zu, align_bytes=64) for zu in pairs}
         grouped = {zu: keep.tile([P, HALF * PACK], BF16, name="grouped%d%d" % zu, align_bytes=64)[:] for zu in pairs}
-        pe_picked = [keep.tile([P, 2, S], F32, name=f"pe_picked{u}") for u in range(2)]
+        pe_picked = keep.tile([P, PACK, S], F32, name="pe_picked")
         h_bf = keep.tile([P, S, PACK], BF16, name="h_bf", align_bytes=64)
         whole = slice(0, S)
         list_halves = [slice(0, S // 2), slice(S // 2, S)]
-        h_bank = {(u, v): psum.tile([P, 2, S // 2], F32, name=f"h_bank{u}{v}") for u in range(2) for v in range(2)}
+        chunks = [slice(CHUNK * c, CHUNK * (c + 1)) for c in range(CHUNKS)]
+        pair_bank = [psum.tile([P, 2, S // 2], F32, name=f"pair_bank{u}") for u in range(2)]
+        chunk_bank = {c: psum.tile([P, PACK, CHUNK], F32, name=f"chunk_bank{c}") for c in (2, 3)}
 
         def round_w1(copy, z, u, raw):
             copy(
@@ -95,21 +97,22 @@ def tile_picked_posadd_none_p_kernel(tc, x_words, x_scales, w1, w2_words, w2_sca
             nc.vector.quantize_mx(out=w1_codes[z, u][:].bitcast(FP8X4), scales=w1_plane[z, u][:], in_=grouped[z, u])
 
         def multiply(z, u, v):
-            cols = list_halves[v]
-            for e in range(2):
-                chans = slice(P * e, P * (e + 1))
-                nc.tensor.matmul_mx(
-                    out=h_bank[u, v][:, e, :],
-                    lhsT=w1_codes[z, u][:, chans].bitcast(FP8X4),
-                    lhsT_scale=w1_plane[z, u][:, chans],
-                    rhs=x_codes[z][:, cols].bitcast(FP8X4),
-                    rhs_scale=x_planes[4 * z :, cols],
-                    start=(z == 0 and e == 0),
-                    stop=(z == PASSES - 1 and e == 1),
-                )
+            for c in [None] if v == 0 else [2, 3]:
+                cols = list_halves[0] if v == 0 else chunks[c]
+                for e in range(2):
+                    chans = slice(P * e, P * (e + 1))
+                    nc.tensor.matmul_mx(
+                        out=pair_bank[u][:, e, :] if v == 0 else chunk_bank[c][:, 2 * u + e, :],
+                        lhsT=w1_codes[z, u][:, chans].bitcast(FP8X4),
+                        lhsT_scale=w1_plane[z, u][:, chans],
+                        rhs=x_codes[z][:, cols].bitcast(FP8X4),
+                        rhs_scale=x_planes[4 * z :, cols],
+                        start=(z == 0 and e == 0 and (v == 0 or u == 0)),
+                        stop=(z == PASSES - 1 and e == 1 and (v == 0 or u == 1)),
+                    )
 
         def pick_pe(engine, t, cols):
-            picked = pe_picked[t // 2][:, t % 2, cols]
+            picked = pe_picked[:, t, cols]
             window = pe_table[t][:].indirect(entries(cols))
             if engine is nc.scalar:
                 nc.scalar.activation(picked, window, COPY)
@@ -117,44 +120,51 @@ def tile_picked_posadd_none_p_kernel(tc, x_words, x_scales, w1, w2_words, w2_sca
                 nc.vector.tensor_copy(picked, window)
 
         def add_pair(u, cols):
-            v = cols.start // (S // 2)
-            in_bank = slice(cols.start - v * S // 2, cols.stop - v * S // 2)
             nc.vector.tensor_tensor(
                 h_bf[:, cols, 2 * u : 2 * u + 2],
-                h_bank[u, v][:, :, in_bank].rearrange("p e c -> p c e"),
-                pe_picked[u][:, :, cols].rearrange("p e c -> p c e"),
+                pair_bank[u][:, :, cols].rearrange("p e c -> p c e"),
+                pe_picked[:, 2 * u : 2 * u + 2, cols].rearrange("p e c -> p c e"),
+                ADD,
+            )
+
+        def add_all(c):
+            nc.vector.tensor_tensor(
+                h_bf[:, chunks[c], :].rearrange("p (b i) t -> p b t i", i=4),
+                chunk_bank[c][:].rearrange("p t (b i) -> p b t i", i=4),
+                pe_picked[:, :, chunks[c]].rearrange("p t (b i) -> p b t i", i=4),
                 ADD,
             )
 
         pick_x(0, whole)
         nc.vector.tensor_copy(x_planes[:], xs_table[:].indirect(offsets[:]))
+        pick_x(1, whole)
         for z, raw in enumerate((w1_first, w1_second)):
             round_w1(nc.vector.tensor_copy, z, 0, raw)
             round_w1(nc.scalar.copy, z, 1, raw)
-            if z == 0:
-                for u in range(2):
-                    quantize_w1(0, u)
-                    for v in range(2):
-                        multiply(0, u, v)
-        quantize_w1(1, 0)
-        for v in range(2):
-            pick_x(1, list_halves[v])
-            multiply(1, 0, v)
-        quantize_w1(1, 1)
-        for v in range(2):
-            multiply(1, 1, v)
+            for u in range(2):
+                quantize_w1(z, u)
+                for v in range(2):
+                    multiply(z, u, v)
+
+        first = chunks[0]
+        first_product = keep.tile([P, 2, CHUNK], F32, name="first_product")
+        first_sum = keep.tile([P, 2, CHUNK], F32, name="first_sum")
+
+        def pick_and_add(e):
+            nc.vector.tensor_tensor(first_sum[:, e, :], pe_table[2 + e][:].indirect(entries(first)), first_product[:, e, :], ADD)
 
         pick_pe(nc.scalar, 0, whole)
-        pick_pe(nc.vector, 1, list_halves[0])
-        pick_pe(nc.scalar, 1, list_halves[1])
-        for cols in list_halves:
-            add_pair(0, cols)
-        pick_pe(nc.scalar, 2, whole)
+        nc.vector.tensor_copy(first_product[:], pair_bank[1][:, :, first])
+        pick_pe(nc.scalar, 1, list_halves[0])
+        pick_pe(nc.vector, 1, chunks[3])
+        pick_pe(nc.scalar, 1, chunks[2])
+        add_pair(0, list_halves[0])
+        pick_pe(nc.scalar, 2, slice(CHUNK, S))
+        pick_and_add(0)
 
         out_rows = out.rearrange("(a p) n -> p a n", p=P)
-        chunks = [slice(CHUNK * c, CHUNK * (c + 1)) for c in range(CHUNKS)]
         o_bank = [psum.tile([P, N // P, CHUNK], F32, name=f"o_bank{c}") for c in range(CHUNKS)]
-        spare = psum.tile([P, CHUNK], F32, name="spare", tag="h_bank00")
+        spare = {c: psum.tile([P, CHUNK], F32, name=f"spare{c}", tag=f"pair_bank{c - 2}") for c in (2, 3)}
 
         def multiply_chunk(c):
             h_codes = keep.tile([P, CHUNK], U32, name=f"h_codes{c}", align_bytes=64)
@@ -164,7 +174,7 @@ def tile_picked_posadd_none_p_kernel(tc, x_words, x_scales, w1, w2_words, w2_sca
             )
             for a in range(N // P):
                 nc.tensor.matmul_mx(
-                    out=spare[:] if (c, a) == (CHUNKS - 1, 0) else o_bank[c][:, a, :],
+                    out=spare[c][:] if c in spare and a == 0 else o_bank[c][:, a, :],
                     lhsT=w2_codes[:, 2 * P * a : 2 * P * (a + 1)].bitcast(FP4X4),
                     lhsT_scale=w2_plane[:, P * a : P * (a + 1)],
                     rhs=h_codes[:].bitcast(FP8X4),
@@ -173,20 +183,23 @@ def tile_picked_posadd_none_p_kernel(tc, x_words, x_scales, w1, w2_words, w2_sca
                     stop=True,
                 )
 
-        for c in range(CHUNKS):
+        pick_and_add(1)
+        pick_pe(nc.scalar, 3, chunks[1])
+        nc.scalar.copy(h_bf[:, first, 2:PACK], first_sum[:].rearrange("p e c -> p c e"))
+        for c in range(2, CHUNKS):
             pick_pe(nc.scalar, 3, chunks[c])
-        for c in range(CHUNKS):
-            add_pair(1, chunks[c])
-            if c > 0:
-                multiply_chunk(c - 1)
+        add_pair(1, chunks[1])
+        multiply_chunk(0)
+        for c in range(2, CHUNKS):
+            add_all(c)
+            multiply_chunk(c - 1)
         multiply_chunk(CHUNKS - 1)
 
         staged = keep.tile([P, N // P, S], F32, name="staged")
-        for c in range(CHUNKS - 1):
-            nc.scalar.copy(staged[:, :, chunks[c]], o_bank[c][:])
-            if c > 0:
-                cols = slice(0, 2 * CHUNK) if c == 1 else chunks[c]
-                nc.sync.dma_start(out=out_rows[:, :, cols], in_=staged[:, :, cols])
-        nc.scalar.copy(staged[:, 0, chunks[-1]], spare[:])
-        nc.vector.tensor_copy(staged[:, 1, chunks[-1]], o_bank[-1][:, 1, :])
-        nc.sync.dma_start(out=out_rows[:, :, chunks[-1]], in_=staged[:, :, chunks[-1]])
+        for c in range(CHUNKS):
+            if c in spare:
+                nc.scalar.copy(staged[:, 0, chunks[c]], spare[c][:])
+                nc.vector.tensor_copy(staged[:, 1, chunks[c]], o_bank[c][:, 1, :])
+            else:
+                nc.scalar.copy(staged[:, :, chunks[c]], o_bank[c][:])
+            nc.sync.dma_start(out=out_rows[:, :, chunks[c]], in_=staged[:, :, chunks[c]])

@@ -31,16 +31,13 @@ def tile_picked_posadd_none_p_kernel(tc, x_words, x_scales, w1, w2_words, w2_sca
         psum = ctx.enter_context(tc.psum_pool(name="psum", bufs=1))
 
         offsets = keep.tile([P, S // 16], U16, name="offsets")
-        x_table = [keep.tile([P, T], I32, name=f"x_table{z}") for z in range(PASSES)]
-        xs_table = keep.tile([P, T], U8, name="xs_table")
+        x_table = [keep.tile([P, T], I32, name=f"x_table{z}", align_bytes=64) for z in range(PASSES)]
+        xs_table = keep.tile([P, T], U8, name="xs_table", align_bytes=64)
         w1_first = keep.tile([P, PACK, H], F32, name="w1_first")
         w1_second = keep.tile([P, PACK, H], F32, name="w1_second")
-        pe_table = [keep.tile([P, T], F32, name=f"pe_table{t}") for t in range(PACK)]
-        w2_codes = keep.tile([P, 2 * N], U8, name="w2_codes", align_bytes=64)
-        w2_plane = keep.tile([P, N], U8, name="w2_plane", align_bytes=64)
-
+        x_planes = keep.tile([P, PASSES, S], U8, name="x_planes", align_bytes=64)
         nc.vector.memset(xs_table[:].bitcast(I32), 0)
-        nc.gpsimd.memset(w2_plane[:].bitcast(I32), 0)
+        nc.gpsimd.memset(x_planes[:].rearrange("p z c -> p (z c)").bitcast(I32), 0)
 
         def load_x(z):
             nc.sync.dma_start(out=x_table[z][:], in_=x_words[z].rearrange("p c r -> p (c r)").bitcast(I32))
@@ -50,25 +47,14 @@ def tile_picked_posadd_none_p_kernel(tc, x_words, x_scales, w1, w2_words, w2_sca
 
         load_x(0)
         nc.sync.dma_start(offsets[:], offs)
-        for q in range(4):
-            nc.sync.dma_start(
-                out=xs_table[32 * q : 32 * q + 4 * PASSES, :].bitcast(I32),
-                in_=x_scales[:, 4 * q : 4 * q + 4, :].bitcast(I32),
-            )
+        for z in range(PASSES):
+            nc.sync.dma_start(out=xs_table[4 * z : P : 8, :].bitcast(I32), in_=x_scales[z].bitcast(I32))
         load_x(1)
         nc.sync.dma_start(out=w1_first[:], in_=w1_rows[0])
         nc.sync.dma_start(out=w1_second[:], in_=w1_rows[1])
-        for t in range(PACK):
-            nc.sync.dma_start(out=pe_table[t][:], in_=pe_rows[:, t, :])
-        nc.sync.dma_start(out=w2_codes[:].bitcast(I32), in_=w2_words[0].bitcast(I32))
-        for q in range(4):
-            nc.sync.dma_start(
-                out=w2_plane[32 * q : 32 * q + 4, :].bitcast(I32),
-                in_=w2_scales[0, 4 * q : 4 * q + 4, :].bitcast(I32),
-            )
 
         x_codes = [keep.tile([P, S], U32, name=f"x_codes{z}", align_bytes=64) for z in range(PASSES)]
-        x_planes = keep.tile([P, S], U8, name="x_planes", align_bytes=64)
+        xs_picked = keep.tile([P, S], U8, name="xs_picked")
         pairs = [(z, u) for z in range(PASSES) for u in range(2)]
         w1_codes = {zu: keep.tile([P, HALF], U32, name="w1_codes%d%d" % zu, align_bytes=64) for zu in pairs}
         w1_plane = {zu: keep.tile([P, HALF], U8, name="w1_plane%d%d" % zu, align_bytes=64) for zu in pairs}
@@ -78,8 +64,11 @@ def tile_picked_posadd_none_p_kernel(tc, x_words, x_scales, w1, w2_words, w2_sca
         whole = slice(0, S)
         list_halves = [slice(0, S // 2), slice(S // 2, S)]
         chunks = [slice(CHUNK * c, CHUNK * (c + 1)) for c in range(CHUNKS)]
-        pair_bank = [psum.tile([P, 2, S // 2], F32, name=f"pair_bank{u}") for u in range(2)]
-        chunk_bank = {c: psum.tile([P, PACK, CHUNK], F32, name=f"chunk_bank{c}") for c in (2, 3)}
+        early = [(0, list_halves[0]), (1, chunks[0]), (1, chunks[1])]
+        pair_bank = {
+            (u, cols.start): psum.tile([P, 2, cols.stop - cols.start], F32, name=f"pair_bank{u}_{cols.start}") for u, cols in early
+        }
+        chunk_bank = {}
 
         def round_w1(copy, z, u, raw):
             copy(
@@ -96,20 +85,30 @@ def tile_picked_posadd_none_p_kernel(tc, x_words, x_scales, w1, w2_words, w2_sca
         def quantize_w1(z, u):
             nc.vector.quantize_mx(out=w1_codes[z, u][:].bitcast(FP8X4), scales=w1_plane[z, u][:], in_=grouped[z, u])
 
-        def multiply(z, u, v):
-            for c in [None] if v == 0 else [2, 3]:
-                cols = list_halves[0] if v == 0 else chunks[c]
-                for e in range(2):
-                    chans = slice(P * e, P * (e + 1))
-                    nc.tensor.matmul_mx(
-                        out=pair_bank[u][:, e, :] if v == 0 else chunk_bank[c][:, 2 * u + e, :],
-                        lhsT=w1_codes[z, u][:, chans].bitcast(FP8X4),
-                        lhsT_scale=w1_plane[z, u][:, chans],
-                        rhs=x_codes[z][:, cols].bitcast(FP8X4),
-                        rhs_scale=x_planes[4 * z :, cols],
-                        start=(z == 0 and e == 0 and (v == 0 or u == 0)),
-                        stop=(z == PASSES - 1 and e == 1 and (v == 0 or u == 1)),
-                    )
+        def multiply(z, t, cols, bank, start, stop):
+            chans = slice(P * (t % 2), P * (t % 2 + 1))
+            nc.tensor.matmul_mx(
+                out=bank,
+                lhsT=w1_codes[z, t // 2][:, chans].bitcast(FP8X4),
+                lhsT_scale=w1_plane[z, t // 2][:, chans],
+                rhs=x_codes[z][:, cols].bitcast(FP8X4),
+                rhs_scale=x_planes[:, z, cols],
+                start=start,
+                stop=stop,
+            )
+
+        def multiply_pair(z, u):
+            for pair, cols in early:
+                if pair == u:
+                    for e in range(2):
+                        bank = pair_bank[u, cols.start][:, e, :]
+                        multiply(z, 2 * u + e, cols, bank, (z, e) == (0, 0), (z, e) == (PASSES - 1, 1))
+
+        def multiply_late(c, tag):
+            chunk_bank[c] = psum.tile([P, PACK, CHUNK], F32, name=f"chunk_bank{c}", tag=tag)
+            for z in range(PASSES):
+                for t in range(PACK):
+                    multiply(z, t, chunks[c], chunk_bank[c][:, t, :], (z, t) == (0, 0), (z, t) == (PASSES - 1, PACK - 1))
 
         def pick_pe(engine, t, cols):
             picked = pe_picked[:, t, cols]
@@ -122,7 +121,7 @@ def tile_picked_posadd_none_p_kernel(tc, x_words, x_scales, w1, w2_words, w2_sca
         def add_pair(u, cols):
             nc.vector.tensor_tensor(
                 h_bf[:, cols, 2 * u : 2 * u + 2],
-                pair_bank[u][:, :, cols].rearrange("p e c -> p c e"),
+                pair_bank[u, cols.start][:].rearrange("p e c -> p c e"),
                 pe_picked[:, 2 * u : 2 * u + 2, cols].rearrange("p e c -> p c e"),
                 ADD,
             )
@@ -136,15 +135,39 @@ def tile_picked_posadd_none_p_kernel(tc, x_words, x_scales, w1, w2_words, w2_sca
             )
 
         pick_x(0, whole)
-        nc.vector.tensor_copy(x_planes[:], xs_table[:].indirect(offsets[:]))
+        nc.vector.tensor_copy(xs_picked[:], xs_table[:].indirect(offsets[:]))
+        for q in range(4):
+            nc.sync.dma_start(
+                out=x_planes[32 * q : 32 * q + 4].rearrange("p z c -> p (z c)").bitcast(I32),
+                in_=xs_picked[32 * q : 32 * (q + 1) : 4, :].bitcast(I32),
+            )
+        pe_table = []
+
+        def load_pe(tag):
+            t = len(pe_table)
+            pe_table.append(keep.tile([P, T], F32, name=f"pe_table{t}", tag=tag, align_bytes=64))
+            nc.sync.dma_start(out=pe_table[t][:], in_=pe_rows[:, t, :])
+
+        load_pe("xs_table")
         pick_x(1, whole)
+        load_pe("x_table1")
         for z, raw in enumerate((w1_first, w1_second)):
             round_w1(nc.vector.tensor_copy, z, 0, raw)
             round_w1(nc.scalar.copy, z, 1, raw)
             for u in range(2):
                 quantize_w1(z, u)
-                for v in range(2):
-                    multiply(z, u, v)
+                if z == 0:
+                    load_pe(f"grouped0{u}")
+                multiply_pair(z, u)
+        w2_codes = keep.tile([P, 2 * N], U8, name="w2_codes", tag="grouped10", align_bytes=64)
+        w2_plane = keep.tile([P, N], U8, name="w2_plane", tag="grouped11", align_bytes=64)
+        nc.sync.dma_start(out=w2_codes[:].bitcast(I32), in_=w2_words[0].bitcast(I32))
+        nc.gpsimd.memset(w2_plane[:].bitcast(I32), 0)
+        for q in range(4):
+            nc.sync.dma_start(
+                out=w2_plane[32 * q : 32 * q + 4, :].bitcast(I32),
+                in_=w2_scales[0, 4 * q : 4 * q + 4, :].bitcast(I32),
+            )
 
         first = chunks[0]
         first_product = keep.tile([P, 2, CHUNK], F32, name="first_product")
@@ -154,17 +177,19 @@ def tile_picked_posadd_none_p_kernel(tc, x_words, x_scales, w1, w2_words, w2_sca
             nc.vector.tensor_tensor(first_sum[:, e, :], pe_table[2 + e][:].indirect(entries(first)), first_product[:, e, :], ADD)
 
         pick_pe(nc.scalar, 0, whole)
-        nc.vector.tensor_copy(first_product[:], pair_bank[1][:, :, first])
+        nc.vector.tensor_copy(first_product[:], pair_bank[1, 0][:])
+        multiply_late(2, "pair_bank1_0")
         pick_pe(nc.scalar, 1, list_halves[0])
         pick_pe(nc.vector, 1, chunks[3])
         pick_pe(nc.scalar, 1, chunks[2])
         add_pair(0, list_halves[0])
+        multiply_late(3, "pair_bank0_0")
         pick_pe(nc.scalar, 2, slice(CHUNK, S))
         pick_and_add(0)
 
         out_rows = out.rearrange("(a p) n -> p a n", p=P)
         o_bank = [psum.tile([P, N // P, CHUNK], F32, name=f"o_bank{c}") for c in range(CHUNKS)]
-        spare = {c: psum.tile([P, CHUNK], F32, name=f"spare{c}", tag=f"pair_bank{c - 2}") for c in (2, 3)}
+        spare = {c: psum.tile([P, CHUNK], F32, name=f"spare{c}", tag="pair_bank1_128" if c == 3 else "spare") for c in (2, 3)}
 
         def multiply_chunk(c):
             h_codes = keep.tile([P, CHUNK], U32, name=f"h_codes{c}", align_bytes=64)

@@ -22,6 +22,7 @@ PASSES = K // (P * PACK)
 HALF = H // 2
 CHUNK = 128
 CHUNKS = S // CHUNK
+VECTOR_ENTRIES = 64
 
 
 def tile_picked_posadd_none_p_kernel(tc, x_words, x_scales, w1, w2_words, w2_scales, pe, offs, out):
@@ -64,11 +65,14 @@ def tile_picked_posadd_none_p_kernel(tc, x_words, x_scales, w1, w2_words, w2_sca
         whole = slice(0, S)
         list_halves = [slice(0, S // 2), slice(S // 2, S)]
         chunks = [slice(CHUNK * c, CHUNK * (c + 1)) for c in range(CHUNKS)]
-        early = [(0, list_halves[0]), (1, chunks[0]), (1, chunks[1])]
-        pair_bank = {
-            (u, cols.start): psum.tile([P, 2, cols.stop - cols.start], F32, name=f"pair_bank{u}_{cols.start}") for u, cols in early
-        }
-        chunk_bank = {}
+        early = [(0, list_halves[0]), (0, list_halves[1]), (1, chunks[0])]
+        pair_bank = {}
+
+        def open_bank(u, cols, tag):
+            pair_bank[u, cols.start, cols.stop] = psum.tile([P, 2, cols.stop - cols.start], F32, name=f"bank{u}_{cols.start}", tag=tag)
+
+        for u, cols in early:
+            open_bank(u, cols, f"early{u}_{cols.start}")
 
         def round_w1(copy, z, u, raw):
             copy(
@@ -97,18 +101,15 @@ def tile_picked_posadd_none_p_kernel(tc, x_words, x_scales, w1, w2_words, w2_sca
                 stop=stop,
             )
 
-        def multiply_pair(z, u):
-            for pair, cols in early:
-                if pair == u:
-                    for e in range(2):
-                        bank = pair_bank[u, cols.start][:, e, :]
-                        multiply(z, 2 * u + e, cols, bank, (z, e) == (0, 0), (z, e) == (PASSES - 1, 1))
+        def multiply_pair(z, u, cols):
+            for e in range(2):
+                bank = pair_bank[u, cols.start, cols.stop][:, e, :]
+                multiply(z, 2 * u + e, cols, bank, (z, e) == (0, 0), (z, e) == (PASSES - 1, 1))
 
-        def multiply_late(c, tag):
-            chunk_bank[c] = psum.tile([P, PACK, CHUNK], F32, name=f"chunk_bank{c}", tag=tag)
+        def multiply_late(cols, tag):
+            open_bank(1, cols, tag)
             for z in range(PASSES):
-                for t in range(PACK):
-                    multiply(z, t, chunks[c], chunk_bank[c][:, t, :], (z, t) == (0, 0), (z, t) == (PASSES - 1, PACK - 1))
+                multiply_pair(z, 1, cols)
 
         def pick_pe(engine, t, cols):
             picked = pe_picked[:, t, cols]
@@ -119,18 +120,11 @@ def tile_picked_posadd_none_p_kernel(tc, x_words, x_scales, w1, w2_words, w2_sca
                 nc.vector.tensor_copy(picked, window)
 
         def add_pair(u, cols):
+            (bank, start), = [(b, lo) for (pair, lo, hi), b in pair_bank.items() if pair == u and lo <= cols.start < hi]
             nc.vector.tensor_tensor(
                 h_bf[:, cols, 2 * u : 2 * u + 2],
-                pair_bank[u, cols.start][:].rearrange("p e c -> p c e"),
+                bank[:, :, cols.start - start : cols.stop - start].rearrange("p e c -> p c e"),
                 pe_picked[:, 2 * u : 2 * u + 2, cols].rearrange("p e c -> p c e"),
-                ADD,
-            )
-
-        def add_all(c):
-            nc.vector.tensor_tensor(
-                h_bf[:, chunks[c], :].rearrange("p (b i) t -> p b t i", i=4),
-                chunk_bank[c][:].rearrange("p t (b i) -> p b t i", i=4),
-                pe_picked[:, :, chunks[c]].rearrange("p t (b i) -> p b t i", i=4),
                 ADD,
             )
 
@@ -158,7 +152,9 @@ def tile_picked_posadd_none_p_kernel(tc, x_words, x_scales, w1, w2_words, w2_sca
                 quantize_w1(z, u)
                 if z == 0:
                     load_pe(f"grouped0{u}")
-                multiply_pair(z, u)
+                for pair, cols in early:
+                    if pair == u:
+                        multiply_pair(z, u, cols)
         w2_codes = keep.tile([P, 2 * N], U8, name="w2_codes", tag="grouped10", align_bytes=64)
         w2_plane = keep.tile([P, N], U8, name="w2_plane", tag="grouped11", align_bytes=64)
         nc.sync.dma_start(out=w2_codes[:].bitcast(I32), in_=w2_words[0].bitcast(I32))
@@ -169,27 +165,19 @@ def tile_picked_posadd_none_p_kernel(tc, x_words, x_scales, w1, w2_words, w2_sca
                 in_=w2_scales[0, 4 * q : 4 * q + 4, :].bitcast(I32),
             )
 
-        first = chunks[0]
-        first_product = keep.tile([P, 2, CHUNK], F32, name="first_product")
-        first_sum = keep.tile([P, 2, CHUNK], F32, name="first_sum")
-
-        def pick_and_add(e):
-            nc.vector.tensor_tensor(first_sum[:, e, :], pe_table[2 + e][:].indirect(entries(first)), first_product[:, e, :], ADD)
-
         pick_pe(nc.scalar, 0, whole)
-        nc.vector.tensor_copy(first_product[:], pair_bank[1, 0][:])
-        multiply_late(2, "pair_bank1_0")
-        pick_pe(nc.scalar, 1, list_halves[0])
-        pick_pe(nc.vector, 1, chunks[3])
-        pick_pe(nc.scalar, 1, chunks[2])
+        pick_pe(nc.vector, 1, list_halves[0])
+        pick_pe(nc.scalar, 1, list_halves[1])
         add_pair(0, list_halves[0])
-        multiply_late(3, "pair_bank0_0")
-        pick_pe(nc.scalar, 2, slice(CHUNK, S))
-        pick_and_add(0)
+        multiply_late(slice(CHUNK, 3 * CHUNK), "early0_0")
+        add_pair(0, list_halves[1])
+        multiply_late(chunks[3], "early0_256")
+        pick_pe(nc.scalar, 2, slice(0, S - VECTOR_ENTRIES))
+        pick_pe(nc.vector, 2, slice(S - VECTOR_ENTRIES, S))
 
         out_rows = out.rearrange("(a p) n -> p a n", p=P)
         o_bank = [psum.tile([P, N // P, CHUNK], F32, name=f"o_bank{c}") for c in range(CHUNKS)]
-        spare = {c: psum.tile([P, CHUNK], F32, name=f"spare{c}", tag="pair_bank1_128" if c == 3 else "spare") for c in (2, 3)}
+        spare = {c: psum.tile([P, CHUNK], F32, name=f"spare{c}", tag="early1_0" if c == 3 else "spare") for c in (2, 3)}
 
         def multiply_chunk(c):
             h_codes = keep.tile([P, CHUNK], U32, name=f"h_codes{c}", align_bytes=64)
@@ -208,16 +196,12 @@ def tile_picked_posadd_none_p_kernel(tc, x_words, x_scales, w1, w2_words, w2_sca
                     stop=True,
                 )
 
-        pick_and_add(1)
-        pick_pe(nc.scalar, 3, chunks[1])
-        nc.scalar.copy(h_bf[:, first, 2:PACK], first_sum[:].rearrange("p e c -> p c e"))
-        for c in range(2, CHUNKS):
+        for c in range(CHUNKS):
             pick_pe(nc.scalar, 3, chunks[c])
-        add_pair(1, chunks[1])
-        multiply_chunk(0)
-        for c in range(2, CHUNKS):
-            add_all(c)
-            multiply_chunk(c - 1)
+        for c in range(CHUNKS):
+            add_pair(1, chunks[c])
+            if c > 0:
+                multiply_chunk(c - 1)
         multiply_chunk(CHUNKS - 1)
 
         staged = keep.tile([P, N // P, S], F32, name="staged")

@@ -22,6 +22,8 @@ PASSES = K // (P * PACK)
 HALF = H // 2
 CHUNK = 128
 CHUNKS = S // CHUNK
+FIRST, SECOND, THIRD, LAST = range(CHUNKS)
+VECTOR_ROUNDS = 40
 VECTOR_ENTRIES = 64
 
 
@@ -34,8 +36,7 @@ def tile_picked_posadd_none_p_kernel(tc, x_words, x_scales, w1, w2_words, w2_sca
         offsets = keep.tile([P, S // 16], U16, name="offsets")
         x_table = [keep.tile([P, T], I32, name=f"x_table{z}", align_bytes=64) for z in range(PASSES)]
         xs_table = keep.tile([P, T], U8, name="xs_table", align_bytes=64)
-        w1_first = keep.tile([P, PACK, H], F32, name="w1_first")
-        w1_second = keep.tile([P, PACK, H], F32, name="w1_second")
+        w1_raw = [keep.tile([P, PACK, H], F32, name=f"w1_raw{z}") for z in range(PASSES)]
         x_planes = keep.tile([P, PASSES, S], U8, name="x_planes", align_bytes=64)
         nc.vector.memset(xs_table[:].bitcast(I32), 0)
         nc.gpsimd.memset(x_planes[:].rearrange("p z c -> p (z c)").bitcast(I32), 0)
@@ -51,8 +52,8 @@ def tile_picked_posadd_none_p_kernel(tc, x_words, x_scales, w1, w2_words, w2_sca
         for z in range(PASSES):
             nc.sync.dma_start(out=xs_table[4 * z : P : 8, :].bitcast(I32), in_=x_scales[z].bitcast(I32))
         load_x(1)
-        nc.sync.dma_start(out=w1_first[:], in_=w1_rows[0])
-        nc.sync.dma_start(out=w1_second[:], in_=w1_rows[1])
+        for z in range(PASSES):
+            nc.sync.dma_start(out=w1_raw[z][:], in_=w1_rows[z])
 
         x_codes = [keep.tile([P, S], U32, name=f"x_codes{z}", align_bytes=64) for z in range(PASSES)]
         xs_picked = keep.tile([P, S], U8, name="xs_picked")
@@ -61,30 +62,20 @@ def tile_picked_posadd_none_p_kernel(tc, x_words, x_scales, w1, w2_words, w2_sca
         w1_plane = {zu: keep.tile([P, HALF], U8, name="w1_plane%d%d" % zu, align_bytes=64) for zu in pairs}
         grouped = {zu: keep.tile([P, HALF * PACK], BF16, name="grouped%d%d" % zu, align_bytes=64)[:] for zu in pairs}
         pe_picked = keep.tile([P, PACK, S], F32, name="pe_picked")
-        h_bf = keep.tile([P, S, PACK], BF16, name="h_bf", align_bytes=64)
-        whole = slice(0, S)
-        list_halves = [slice(0, S // 2), slice(S // 2, S)]
+        h_bf = [keep.tile([P, PACK * CHUNK], BF16, name=f"h_bf{c}", align_bytes=64) for c in range(CHUNKS)]
         chunks = [slice(CHUNK * c, CHUNK * (c + 1)) for c in range(CHUNKS)]
-        early = [(0, list_halves[0]), (0, list_halves[1]), (1, chunks[0])]
-        pair_bank = {}
 
-        def open_bank(u, cols, tag):
-            pair_bank[u, cols.start, cols.stop] = psum.tile([P, 2, cols.stop - cols.start], F32, name=f"bank{u}_{cols.start}", tag=tag)
-
-        for u, cols in early:
-            open_bank(u, cols, f"early{u}_{cols.start}")
-
-        def round_w1(copy, z, u, raw):
+        def round_w1(copy, z, u, ms):
             copy(
-                grouped[z, u].rearrange("p (t m j) -> p m j t", t=2, j=PACK),
-                raw[:].rearrange("p j (m t) -> p m j t", t=PACK)[:, :, :, 2 * u : 2 * u + 2],
+                grouped[z, u].rearrange("p (t m j) -> p m j t", t=2, j=PACK)[:, ms],
+                w1_raw[z][:].rearrange("p j (m t) -> p m j t", t=PACK)[:, ms, :, 2 * u : 2 * u + 2],
             )
 
         def entries(cols):
             return offsets[:, cols.start // 16 : cols.stop // 16]
 
-        def pick_x(z, cols):
-            nc.vector.tensor_copy(x_codes[z][:, cols], x_table[z][:].bitcast(U32).indirect(entries(cols)))
+        def pick_x(z):
+            nc.vector.tensor_copy(x_codes[z][:], x_table[z][:].bitcast(U32).indirect(offsets[:]))
 
         def quantize_w1(z, u):
             nc.vector.quantize_mx(out=w1_codes[z, u][:].bitcast(FP8X4), scales=w1_plane[z, u][:], in_=grouped[z, u])
@@ -101,34 +92,61 @@ def tile_picked_posadd_none_p_kernel(tc, x_words, x_scales, w1, w2_words, w2_sca
                 stop=stop,
             )
 
-        def multiply_pair(z, u, cols):
-            for e in range(2):
-                bank = pair_bank[u, cols.start, cols.stop][:, e, :]
-                multiply(z, 2 * u + e, cols, bank, (z, e) == (0, 0), (z, e) == (PASSES - 1, 1))
+        product = {}
 
-        def multiply_late(cols, tag):
-            open_bank(1, cols, tag)
-            for z in range(PASSES):
-                multiply_pair(z, 1, cols)
+        def open_bank(tag, pieces):
+            width = sum(cols.stop - cols.start for t, cols in pieces)
+            bank = psum.tile([P, width], F32, name="bank%d_%d" % (pieces[0][0], pieces[0][1].start), tag=tag)
+            placed, at = [], 0
+            for t, cols in pieces:
+                n = cols.stop - cols.start
+                placed.append((t, cols, bank[:, at : at + n]))
+                for c in range(cols.start // CHUNK, cols.stop // CHUNK):
+                    lo = at + CHUNK * c - cols.start
+                    product[t, c] = bank[:, lo : lo + CHUNK]
+                at = at + n
+            return bank, placed
+
+        def multiply_bank(z, placed):
+            for i, (t, cols, ap) in enumerate(placed):
+                multiply(z, t, cols, ap, (z, i) == (0, 0), (z, i) == (PASSES - 1, len(placed) - 1))
 
         def pick_pe(engine, t, cols):
-            picked = pe_picked[:, t, cols]
             window = pe_table[t][:].indirect(entries(cols))
             if engine is nc.scalar:
-                nc.scalar.activation(picked, window, COPY)
+                nc.scalar.activation(pe_picked[:, t, cols], window, COPY)
             else:
-                nc.vector.tensor_copy(picked, window)
+                nc.vector.tensor_copy(pe_picked[:, t, cols], window)
 
-        def add_pair(u, cols):
-            (bank, start), = [(b, lo) for (pair, lo, hi), b in pair_bank.items() if pair == u and lo <= cols.start < hi]
+        def add_pair(u, c, part=slice(0, CHUNK)):
             nc.vector.tensor_tensor(
-                h_bf[:, cols, 2 * u : 2 * u + 2],
-                bank[:, :, cols.start - start : cols.stop - start].rearrange("p e c -> p c e"),
-                pe_picked[:, 2 * u : 2 * u + 2, cols].rearrange("p e c -> p c e"),
+                h_bf[c][:].rearrange("p (n t) -> p n t", t=PACK)[:, part, 2 * u : 2 * u + 2],
+                pair_product[u, c].rearrange("p e n -> p n e")[:, part],
+                pe_picked[:, 2 * u : 2 * u + 2, chunks[c]].rearrange("p e n -> p n e")[:, part],
                 ADD,
             )
 
-        pick_x(0, whole)
+        list_halves = [slice(0, S // 2), slice(S // 2, S)]
+        pair_product = {}
+
+        def open_pair_bank(tag, u, cols):
+            bank, placed = open_bank(tag, [(t, cols) for t in (2 * u, 2 * u + 1)])
+            for c in range(cols.start // CHUNK, cols.stop // CHUNK):
+                lo = CHUNK * c - cols.start
+                pair_product[u, c] = bank[:].rearrange("p (e n) -> p e n", e=2)[:, :, lo : lo + CHUNK]
+            return placed
+
+        def multiply_late(tag, cols):
+            placed = open_pair_bank(tag, 1, cols)
+            for z in range(PASSES):
+                multiply_bank(z, placed)
+
+        early = {
+            0: [open_pair_bank("low1", 0, list_halves[1]), open_pair_bank("low0", 0, list_halves[0])],
+            1: [open_pair_bank("high", 1, chunks[FIRST])],
+        }
+
+        pick_x(0)
         nc.vector.tensor_copy(xs_picked[:], xs_table[:].indirect(offsets[:]))
         for q in range(4):
             nc.sync.dma_start(
@@ -143,18 +161,20 @@ def tile_picked_posadd_none_p_kernel(tc, x_words, x_scales, w1, w2_words, w2_sca
             nc.sync.dma_start(out=pe_table[t][:], in_=pe_rows[:, t, :])
 
         load_pe("xs_table")
-        pick_x(1, whole)
+        pick_x(1)
         load_pe("x_table1")
-        for z, raw in enumerate((w1_first, w1_second)):
-            round_w1(nc.vector.tensor_copy, z, 0, raw)
-            round_w1(nc.scalar.copy, z, 1, raw)
+        for z in range(PASSES):
+            shared = VECTOR_ROUNDS if z == PASSES - 1 else 0
+            round_w1(nc.vector.tensor_copy, z, 0, slice(0, P))
+            round_w1(nc.scalar.copy, z, 1, slice(shared, P))
+            if shared:
+                round_w1(nc.vector.tensor_copy, z, 1, slice(0, shared))
             for u in range(2):
                 quantize_w1(z, u)
                 if z == 0:
                     load_pe(f"grouped0{u}")
-                for pair, cols in early:
-                    if pair == u:
-                        multiply_pair(z, u, cols)
+                for placed in early[u]:
+                    multiply_bank(z, placed)
         w2_codes = keep.tile([P, 2 * N], U8, name="w2_codes", tag="grouped10", align_bytes=64)
         w2_plane = keep.tile([P, N], U8, name="w2_plane", tag="grouped11", align_bytes=64)
         nc.sync.dma_start(out=w2_codes[:].bitcast(I32), in_=w2_words[0].bitcast(I32))
@@ -165,29 +185,40 @@ def tile_picked_posadd_none_p_kernel(tc, x_words, x_scales, w1, w2_words, w2_sca
                 in_=w2_scales[0, 4 * q : 4 * q + 4, :].bitcast(I32),
             )
 
-        pick_pe(nc.scalar, 0, whole)
-        pick_pe(nc.vector, 1, list_halves[0])
-        pick_pe(nc.scalar, 1, list_halves[1])
-        add_pair(0, list_halves[0])
-        multiply_late(slice(CHUNK, 3 * CHUNK), "early0_0")
-        add_pair(0, list_halves[1])
-        multiply_late(chunks[3], "early0_256")
+        pick_pe(nc.scalar, 0, slice(0, S - CHUNK))
+        pick_pe(nc.vector, 0, chunks[LAST])
+        pick_pe(nc.vector, 1, chunks[LAST])
+        pick_pe(nc.vector, 1, slice(S - CHUNK - VECTOR_ENTRIES, S - CHUNK))
+        for cols in (slice(2 * CHUNK, S - CHUNK - VECTOR_ENTRIES), chunks[0], chunks[1]):
+            pick_pe(nc.scalar, 1, cols)
+        for c in (LAST, THIRD):
+            add_pair(0, c)
+        multiply_late("low1", chunks[SECOND])
+        for c in (FIRST, SECOND):
+            add_pair(0, c)
+        multiply_late("low0", list_halves[1])
+
         pick_pe(nc.scalar, 2, slice(0, S - VECTOR_ENTRIES))
         pick_pe(nc.vector, 2, slice(S - VECTOR_ENTRIES, S))
 
         out_rows = out.rearrange("(a p) n -> p a n", p=P)
-        o_bank = [psum.tile([P, N // P, CHUNK], F32, name=f"o_bank{c}") for c in range(CHUNKS)]
-        spare = {c: psum.tile([P, CHUNK], F32, name=f"spare{c}", tag="early1_0" if c == 3 else "spare") for c in (2, 3)}
+        staged = keep.tile([P, N // P, S], F32, name="staged")
+        freed = {(LAST, 1): "high"}
+        o_bank = {}
 
         def multiply_chunk(c):
             h_codes = keep.tile([P, CHUNK], U32, name=f"h_codes{c}", align_bytes=64)
             h_plane = keep.tile([P, CHUNK], U8, name=f"h_plane{c}", align_bytes=64)
-            nc.vector.quantize_mx(
-                out=h_codes[:].bitcast(FP8X4), scales=h_plane[:], in_=h_bf[:, chunks[c], :].rearrange("p c t -> p (c t)")
-            )
+            nc.vector.quantize_mx(out=h_codes[:].bitcast(FP8X4), scales=h_plane[:], in_=h_bf[c][:])
+            if c in (FIRST, SECOND):
+                o_bank[c] = psum.tile([P, N // P, CHUNK], F32, name=f"o_bank{c}")
             for a in range(N // P):
+                if c in (FIRST, SECOND):
+                    o_bank[c, a] = o_bank[c][:, a, :]
+                else:
+                    o_bank[c, a] = psum.tile([P, CHUNK], F32, name=f"o_bank{c}{a}", tag=freed.get((c, a), f"o_bank{c}{a}"))[:]
                 nc.tensor.matmul_mx(
-                    out=spare[c][:] if c in spare and a == 0 else o_bank[c][:, a, :],
+                    out=o_bank[c, a],
                     lhsT=w2_codes[:, 2 * P * a : 2 * P * (a + 1)].bitcast(FP4X4),
                     lhsT_scale=w2_plane[:, P * a : P * (a + 1)],
                     rhs=h_codes[:].bitcast(FP8X4),
@@ -196,19 +227,26 @@ def tile_picked_posadd_none_p_kernel(tc, x_words, x_scales, w1, w2_words, w2_sca
                     stop=True,
                 )
 
-        for c in range(CHUNKS):
-            pick_pe(nc.scalar, 3, chunks[c])
-        for c in range(CHUNKS):
-            add_pair(1, chunks[c])
-            if c > 0:
-                multiply_chunk(c - 1)
-        multiply_chunk(CHUNKS - 1)
-
-        staged = keep.tile([P, N // P, S], F32, name="staged")
-        for c in range(CHUNKS):
-            if c in spare:
-                nc.scalar.copy(staged[:, 0, chunks[c]], spare[c][:])
-                nc.vector.tensor_copy(staged[:, 1, chunks[c]], o_bank[c][:, 1, :])
-            else:
-                nc.scalar.copy(staged[:, :, chunks[c]], o_bank[c][:])
+        def store_whole(c):
+            nc.scalar.copy(staged[:, :, chunks[c]], o_bank[c][:])
             nc.sync.dma_start(out=out_rows[:, :, chunks[c]], in_=staged[:, :, chunks[c]])
+
+        def store_shared(c):
+            nc.scalar.copy(staged[:, 0, chunks[c]], o_bank[c, 0])
+            nc.vector.tensor_copy(staged[:, 1, chunks[c]], o_bank[c, 1])
+            nc.sync.dma_start(out=out_rows[:, :, chunks[c]], in_=staged[:, :, chunks[c]])
+
+        opening = [slice(0, CHUNK // 2), slice(CHUNK // 2, CHUNK)]
+        pick_pe(nc.vector, 3, slice(2 * CHUNK - VECTOR_ENTRIES, 2 * CHUNK))
+        for cols in opening + [slice(CHUNK, 2 * CHUNK - VECTOR_ENTRIES)] + chunks[2:]:
+            pick_pe(nc.scalar, 3, cols)
+        for part in opening:
+            add_pair(1, FIRST, part)
+        for c in range(1, CHUNKS):
+            add_pair(1, c)
+            multiply_chunk(c - 1)
+        multiply_chunk(LAST)
+        store_whole(FIRST)
+        store_whole(SECOND)
+        store_shared(THIRD)
+        store_shared(LAST)

@@ -193,10 +193,10 @@ def tile_picked_posadd_none_p_kernel(tc, x_words, x_scales, w1, w2_words, w2_sca
             pick_pe(nc.scalar, 1, cols)
         for c in (LAST, THIRD):
             add_pair(0, c)
-        multiply_late("low1", chunks[SECOND])
+        multiply_late("low1", slice(chunks[SECOND].start, chunks[THIRD].stop))
         for c in (FIRST, SECOND):
             add_pair(0, c)
-        multiply_late("low0", list_halves[1])
+        multiply_late("low0", chunks[LAST])
 
         pick_pe(nc.scalar, 2, slice(0, S - VECTOR_ENTRIES))
         pick_pe(nc.vector, 2, slice(S - VECTOR_ENTRIES, S))

@@ -62,6 +62,7 @@ def tile_picked_posadd_none_p_kernel(tc, x_words, x_scales, w1, w2_words, w2_sca
         w1_plane = {zu: keep.tile([P, HALF], U8, name="w1_plane%d%d" % zu, align_bytes=64) for zu in pairs}
         grouped = {zu: keep.tile([P, HALF * PACK], BF16, name="grouped%d%d" % zu, align_bytes=64)[:] for zu in pairs}
         pe_picked = keep.tile([P, PACK, S], F32, name="pe_picked")
+        h_pairs = {c: keep.tile([P, PACK * CHUNK], BF16, name=f"h_pairs{c}") for c in (SECOND, THIRD)}
         h_bf = [keep.tile([P, PACK * CHUNK], BF16, name=f"h_bf{c}", align_bytes=64) for c in range(CHUNKS)]
         chunks = [slice(CHUNK * c, CHUNK * (c + 1)) for c in range(CHUNKS)]
 
@@ -119,8 +120,12 @@ def tile_picked_posadd_none_p_kernel(tc, x_words, x_scales, w1, w2_words, w2_sca
                 nc.vector.tensor_copy(pe_picked[:, t, cols], window)
 
         def add_pair(u, c, part=slice(0, CHUNK)):
+            if c in h_pairs:
+                sums = h_pairs[c][:].rearrange("p (u n e) -> p u n e", u=2, e=2)[:, u]
+            else:
+                sums = h_bf[c][:].rearrange("p (n t) -> p n t", t=PACK)[:, :, 2 * u : 2 * u + 2]
             nc.vector.tensor_tensor(
-                h_bf[c][:].rearrange("p (n t) -> p n t", t=PACK)[:, part, 2 * u : 2 * u + 2],
+                sums[:, part],
                 pair_product[u, c].rearrange("p e n -> p n e")[:, part],
                 pe_picked[:, 2 * u : 2 * u + 2, chunks[c]].rearrange("p e n -> p n e")[:, part],
                 ADD,
@@ -203,17 +208,23 @@ def tile_picked_posadd_none_p_kernel(tc, x_words, x_scales, w1, w2_words, w2_sca
 
         out_rows = out.rearrange("(a p) n -> p a n", p=P)
         staged = keep.tile([P, N // P, S], F32, name="staged")
-        freed = {(LAST, 1): "high"}
+        freed = {(LAST, 0): "low1", (LAST, 1): "high"}
         o_bank = {}
+
+        def interleave(c):
+            nc.scalar.copy(
+                h_bf[c][:].bitcast(U32).rearrange("p (n u) -> p n u", u=2),
+                h_pairs[c][:].bitcast(U32).rearrange("p (u n) -> p n u", u=2),
+            )
 
         def multiply_chunk(c):
             h_codes = keep.tile([P, CHUNK], U32, name=f"h_codes{c}", align_bytes=64)
             h_plane = keep.tile([P, CHUNK], U8, name=f"h_plane{c}", align_bytes=64)
             nc.vector.quantize_mx(out=h_codes[:].bitcast(FP8X4), scales=h_plane[:], in_=h_bf[c][:])
-            if c in (FIRST, SECOND):
+            if c == FIRST:
                 o_bank[c] = psum.tile([P, N // P, CHUNK], F32, name=f"o_bank{c}")
             for a in range(N // P):
-                if c in (FIRST, SECOND):
+                if c == FIRST:
                     o_bank[c, a] = o_bank[c][:, a, :]
                 else:
                     o_bank[c, a] = psum.tile([P, CHUNK], F32, name=f"o_bank{c}{a}", tag=freed.get((c, a), f"o_bank{c}{a}"))[:]
@@ -231,10 +242,12 @@ def tile_picked_posadd_none_p_kernel(tc, x_words, x_scales, w1, w2_words, w2_sca
             nc.scalar.copy(staged[:, :, chunks[c]], o_bank[c][:])
             nc.sync.dma_start(out=out_rows[:, :, chunks[c]], in_=staged[:, :, chunks[c]])
 
-        def store_shared(c):
-            nc.scalar.copy(staged[:, 0, chunks[c]], o_bank[c, 0])
-            nc.vector.tensor_copy(staged[:, 1, chunks[c]], o_bank[c, 1])
-            nc.sync.dma_start(out=out_rows[:, :, chunks[c]], in_=staged[:, :, chunks[c]])
+        def store_shared(group):
+            for c in group:
+                nc.scalar.copy(staged[:, 0, chunks[c]], o_bank[c, 0])
+                nc.vector.tensor_copy(staged[:, 1, chunks[c]], o_bank[c, 1])
+            cols = slice(chunks[group[0]].start, chunks[group[-1]].stop)
+            nc.sync.dma_start(out=out_rows[:, :, cols], in_=staged[:, :, cols])
 
         opening = [slice(0, CHUNK // 2), slice(CHUNK // 2, CHUNK)]
         pick_pe(nc.vector, 3, slice(2 * CHUNK - VECTOR_ENTRIES, 2 * CHUNK))
@@ -242,11 +255,14 @@ def tile_picked_posadd_none_p_kernel(tc, x_words, x_scales, w1, w2_words, w2_sca
             pick_pe(nc.scalar, 3, cols)
         for part in opening:
             add_pair(1, FIRST, part)
-        for c in range(1, CHUNKS):
-            add_pair(1, c)
-            multiply_chunk(c - 1)
-        multiply_chunk(LAST)
+        add_pair(1, SECOND)
+        interleave(SECOND)
+        multiply_chunk(FIRST)
+        add_pair(1, THIRD)
+        interleave(THIRD)
+        add_pair(1, LAST)
+        for c in (SECOND, THIRD, LAST):
+            multiply_chunk(c)
         store_whole(FIRST)
-        store_whole(SECOND)
-        store_shared(THIRD)
-        store_shared(LAST)
+        store_shared([SECOND])
+        store_shared([THIRD, LAST])

@@ -255,6 +255,17 @@ def tile_picked_posadd_none_p_kernel(tc, x_words, x_scales, w1, w2_words, w2_sca
             pick_pe(nc.scalar, 3, cols)
         for part in opening:
             add_pair(1, FIRST, part)
+        unread = psum.tile([P, 2, HALF], F32, name="unread", tag="high")
+        for z in range(PASSES):
+            nc.tensor.matmul_mx(
+                out=unread[:, z, :],
+                lhsT=w1_codes[z, 0][:, :P].bitcast(FP8X4),
+                lhsT_scale=w1_plane[z, 0][:, :P],
+                rhs=w1_codes[z, 1][:].bitcast(FP8X4),
+                rhs_scale=w1_plane[z, 1][:],
+                start=True,
+                stop=True,
+            )
         add_pair(1, SECOND)
         interleave(SECOND)
         multiply_chunk(FIRST)

@@ -198,13 +198,13 @@ def tile_picked_posadd_none_p_kernel(tc, x_words, x_scales, w1, w2_words, w2_sca
             pick_pe(nc.scalar, 1, cols)
         for c in (LAST, THIRD):
             add_pair(0, c)
-        multiply_late("low1", slice(chunks[SECOND].start, chunks[THIRD].stop))
+        multiply_late("low1", chunks[SECOND])
         for c in (FIRST, SECOND):
             add_pair(0, c)
-        multiply_late("low0", chunks[LAST])
+        multiply_late("low0", list_halves[1])
 
-        pick_pe(nc.scalar, 2, slice(0, S - VECTOR_ENTRIES))
-        pick_pe(nc.vector, 2, slice(S - VECTOR_ENTRIES, S))
+        pick_pe(nc.scalar, 2, slice(0, S - CHUNK))
+        pick_pe(nc.vector, 2, chunks[LAST])
 
         out_rows = out.rearrange("(a p) n -> p a n", p=P)
         staged = keep.tile([P, N // P, S], F32, name="staged")

@@ -242,6 +242,11 @@ def tile_picked_posadd_none_p_kernel(tc, x_words, x_scales, w1, w2_words, w2_sca
             nc.scalar.copy(staged[:, :, chunks[c]], o_bank[c][:])
             nc.sync.dma_start(out=out_rows[:, :, chunks[c]], in_=staged[:, :, chunks[c]])
 
+        def store_halves(c):
+            for a, copy in enumerate((nc.scalar.copy, nc.vector.tensor_copy)):
+                copy(staged[:, a, chunks[c]], o_bank[c, a])
+                nc.sync.dma_start(out=out_rows[:, a, chunks[c]], in_=staged[:, a, chunks[c]])
+
         def store_shared(group):
             for c in group:
                 nc.scalar.copy(staged[:, 0, chunks[c]], o_bank[c, 0])
@@ -275,5 +280,5 @@ def tile_picked_posadd_none_p_kernel(tc, x_words, x_scales, w1, w2_words, w2_sca
         for c in (SECOND, THIRD, LAST):
             multiply_chunk(c)
         store_whole(FIRST)
-        store_shared([SECOND])
+        store_halves(SECOND)
         store_shared([THIRD, LAST])

@@ -248,7 +248,7 @@ def tile_picked_posadd_none_p_kernel(tc, x_words, x_scales, w1, w2_words, w2_sca
                 nc.sync.dma_start(out=out_rows[:, a, chunks[c]], in_=staged[:, a, chunks[c]])
 
         def store_shared(group):
-            for c in group:
+            for c in reversed(group):
                 nc.scalar.copy(staged[:, 0, chunks[c]], o_bank[c, 0])
                 nc.vector.tensor_copy(staged[:, 1, chunks[c]], o_bank[c, 1])
             cols = slice(chunks[group[0]].start, chunks[group[-1]].stop)
@@ -277,7 +277,7 @@ def tile_picked_posadd_none_p_kernel(tc, x_words, x_scales, w1, w2_words, w2_sca
         add_pair(1, THIRD)
         interleave(THIRD)
         add_pair(1, LAST)
-        for c in (SECOND, THIRD, LAST):
+        for c in (SECOND, LAST, THIRD):
             multiply_chunk(c)
         store_whole(FIRST)
         store_halves(SECOND)

@@ -49,8 +49,7 @@ def tile_picked_posadd_none_p_kernel(tc, x_words, x_scales, w1, w2_words, w2_sca
 
         load_x(0)
         nc.sync.dma_start(offsets[:], offs)
-        for z in range(PASSES):
-            nc.sync.dma_start(out=xs_table[4 * z : P : 8, :].bitcast(I32), in_=x_scales[z].bitcast(I32))
+        nc.sync.dma_start(out=xs_table[0:P:4, :].bitcast(I32), in_=x_scales.bitcast(I32).rearrange("z q c -> q z c"))
         load_x(1)
         for z in range(PASSES):
             nc.sync.dma_start(out=w1_raw[z][:], in_=w1_rows[z])
@@ -208,7 +207,7 @@ def tile_picked_posadd_none_p_kernel(tc, x_words, x_scales, w1, w2_words, w2_sca
 
         out_rows = out.rearrange("(a p) n -> p a n", p=P)
         staged = keep.tile([P, N // P, S], F32, name="staged")
-        freed = {(LAST, 0): "low1", (LAST, 1): "high"}
+        freed = {(LAST, 0): "low1", (LAST, 1): "high", (THIRD, 1): "low0"}
         o_bank = {}
 
         def interleave(c):
@@ -221,13 +220,8 @@ def tile_picked_posadd_none_p_kernel(tc, x_words, x_scales, w1, w2_words, w2_sca
             h_codes = keep.tile([P, CHUNK], U32, name=f"h_codes{c}", align_bytes=64)
             h_plane = keep.tile([P, CHUNK], U8, name=f"h_plane{c}", align_bytes=64)
             nc.vector.quantize_mx(out=h_codes[:].bitcast(FP8X4), scales=h_plane[:], in_=h_bf[c][:])
-            if c == FIRST:
-                o_bank[c] = psum.tile([P, N // P, CHUNK], F32, name=f"o_bank{c}")
             for a in range(N // P):
-                if c == FIRST:
-                    o_bank[c, a] = o_bank[c][:, a, :]
-                else:
-                    o_bank[c, a] = psum.tile([P, CHUNK], F32, name=f"o_bank{c}{a}", tag=freed.get((c, a), f"o_bank{c}{a}"))[:]
+                o_bank[c, a] = psum.tile([P, CHUNK], F32, name=f"o_bank{c}{a}", tag=freed.get((c, a), f"o_bank{c}{a}"))[:]
                 nc.tensor.matmul_mx(
                     out=o_bank[c, a],
                     lhsT=w2_codes[:, 2 * P * a : 2 * P * (a + 1)].bitcast(FP4X4),
@@ -238,12 +232,8 @@ def tile_picked_posadd_none_p_kernel(tc, x_words, x_scales, w1, w2_words, w2_sca
                     stop=True,
                 )
 
-        def store_whole(c):
-            nc.scalar.copy(staged[:, :, chunks[c]], o_bank[c][:])
-            nc.sync.dma_start(out=out_rows[:, :, chunks[c]], in_=staged[:, :, chunks[c]])
-
-        def store_halves(c):
-            for a, copy in enumerate((nc.scalar.copy, nc.vector.tensor_copy)):
+        def store_halves(c, copies):
+            for a, copy in enumerate(copies):
                 copy(staged[:, a, chunks[c]], o_bank[c, a])
                 nc.sync.dma_start(out=out_rows[:, a, chunks[c]], in_=staged[:, a, chunks[c]])
 
@@ -279,6 +269,6 @@ def tile_picked_posadd_none_p_kernel(tc, x_words, x_scales, w1, w2_words, w2_sca
         add_pair(1, LAST)
         for c in (SECOND, LAST, THIRD):
             multiply_chunk(c)
-        store_whole(FIRST)
-        store_halves(SECOND)
+        store_halves(FIRST, [nc.scalar.copy, nc.scalar.copy])
+        store_halves(SECOND, [nc.scalar.copy, nc.vector.tensor_copy])
         store_shared([THIRD, LAST])

@@ -25,6 +25,7 @@ CHUNKS = S // CHUNK
 FIRST, SECOND, THIRD, LAST = range(CHUNKS)
 VECTOR_ROUNDS = 40
 VECTOR_ENTRIES = 64
+ALIGN = 256
 
 
 def tile_picked_posadd_none_p_kernel(tc, x_words, x_scales, w1, w2_words, w2_scales, pe, offs, out):
@@ -33,11 +34,11 @@ def tile_picked_posadd_none_p_kernel(tc, x_words, x_scales, w1, w2_words, w2_sca
         keep = ctx.enter_context(tc.tile_pool(name="keep", bufs=1))
         psum = ctx.enter_context(tc.psum_pool(name="psum", bufs=1))
 
-        offsets = keep.tile([P, S // 16], U16, name="offsets")
-        x_table = [keep.tile([P, T], I32, name=f"x_table{z}", align_bytes=64) for z in range(PASSES)]
-        xs_table = keep.tile([P, T], U8, name="xs_table", align_bytes=64)
-        w1_raw = [keep.tile([P, PACK, H], F32, name=f"w1_raw{z}") for z in range(PASSES)]
-        x_planes = keep.tile([P, PASSES, S], U8, name="x_planes", align_bytes=64)
+        offsets = keep.tile([P, S // 16], U16, name="offsets", align_bytes=ALIGN)
+        x_table = [keep.tile([P, T], I32, name=f"x_table{z}", align_bytes=ALIGN) for z in range(PASSES)]
+        xs_table = keep.tile([P, T], U8, name="xs_table", align_bytes=ALIGN)
+        w1_raw = [keep.tile([P, PACK, H], F32, name=f"w1_raw{z}", align_bytes=ALIGN) for z in range(PASSES)]
+        x_planes = keep.tile([P, PASSES, S], U8, name="x_planes", align_bytes=ALIGN)
         nc.vector.memset(xs_table[:].bitcast(I32), 0)
         nc.gpsimd.memset(x_planes[:].rearrange("p z c -> p (z c)").bitcast(I32), 0)
 
@@ -54,15 +55,15 @@ def tile_picked_posadd_none_p_kernel(tc, x_words, x_scales, w1, w2_words, w2_sca
         for z in range(PASSES):
             nc.sync.dma_start(out=w1_raw[z][:], in_=w1_rows[z])
 
-        x_codes = [keep.tile([P, S], U32, name=f"x_codes{z}", align_bytes=64) for z in range(PASSES)]
-        xs_picked = keep.tile([P, S], U8, name="xs_picked")
+        x_codes = [keep.tile([P, S], U32, name=f"x_codes{z}", align_bytes=ALIGN) for z in range(PASSES)]
+        xs_picked = keep.tile([P, S], U8, name="xs_picked", align_bytes=ALIGN)
         pairs = [(z, u) for z in range(PASSES) for u in range(2)]
-        w1_codes = {zu: keep.tile([P, HALF], U32, name="w1_codes%d%d" % zu, align_bytes=64) for zu in pairs}
-        w1_plane = {zu: keep.tile([P, HALF], U8, name="w1_plane%d%d" % zu, align_bytes=64) for zu in pairs}
-        grouped = {zu: keep.tile([P, HALF * PACK], BF16, name="grouped%d%d" % zu, align_bytes=64)[:] for zu in pairs}
-        pe_picked = keep.tile([P, PACK, S], F32, name="pe_picked")
-        h_pairs = {c: keep.tile([P, PACK * CHUNK], BF16, name=f"h_pairs{c}") for c in (SECOND, THIRD)}
-        h_bf = [keep.tile([P, PACK * CHUNK], BF16, name=f"h_bf{c}", align_bytes=64) for c in range(CHUNKS)]
+        w1_codes = {zu: keep.tile([P, HALF], U32, name="w1_codes%d%d" % zu, align_bytes=ALIGN) for zu in pairs}
+        w1_plane = {zu: keep.tile([P, HALF], U8, name="w1_plane%d%d" % zu, align_bytes=ALIGN) for zu in pairs}
+        grouped = {zu: keep.tile([P, HALF * PACK], BF16, name="grouped%d%d" % zu, align_bytes=ALIGN)[:] for zu in pairs}
+        pe_picked = keep.tile([P, PACK, S], F32, name="pe_picked", align_bytes=ALIGN)
+        h_pairs = {c: keep.tile([P, PACK * CHUNK], BF16, name=f"h_pairs{c}", align_bytes=ALIGN) for c in (SECOND, THIRD)}
+        h_bf = [keep.tile([P, PACK * CHUNK], BF16, name=f"h_bf{c}", align_bytes=ALIGN) for c in range(CHUNKS)]
         chunks = [slice(CHUNK * c, CHUNK * (c + 1)) for c in range(CHUNKS)]
 
         def round_w1(copy, z, u, ms):
@@ -161,7 +162,7 @@ def tile_picked_posadd_none_p_kernel(tc, x_words, x_scales, w1, w2_words, w2_sca
 
         def load_pe(tag):
             t = len(pe_table)
-            pe_table.append(keep.tile([P, T], F32, name=f"pe_table{t}", tag=tag, align_bytes=64))
+            pe_table.append(keep.tile([P, T], F32, name=f"pe_table{t}", tag=tag, align_bytes=ALIGN))
             nc.sync.dma_start(out=pe_table[t][:], in_=pe_rows[:, t, :])
 
         load_pe("xs_table")
@@ -179,8 +180,8 @@ def tile_picked_posadd_none_p_kernel(tc, x_words, x_scales, w1, w2_words, w2_sca
                     load_pe(f"grouped0{u}")
                 for placed in early[u]:
                     multiply_bank(z, placed)
-        w2_codes = keep.tile([P, 2 * N], U8, name="w2_codes", tag="grouped10", align_bytes=64)
-        w2_plane = keep.tile([P, N], U8, name="w2_plane", tag="grouped11", align_bytes=64)
+        w2_codes = keep.tile([P, 2 * N], U8, name="w2_codes", tag="grouped10", align_bytes=ALIGN)
+        w2_plane = keep.tile([P, N], U8, name="w2_plane", tag="grouped11", align_bytes=ALIGN)
         nc.sync.dma_start(out=w2_codes[:].bitcast(I32), in_=w2_words[0].bitcast(I32))
         nc.gpsimd.memset(w2_plane[:].bitcast(I32), 0)
         for q in range(4):
@@ -206,7 +207,7 @@ def tile_picked_posadd_none_p_kernel(tc, x_words, x_scales, w1, w2_words, w2_sca
         pick_pe(nc.vector, 2, chunks[LAST])
 
         out_rows = out.rearrange("(a p) n -> p a n", p=P)
-        staged = keep.tile([P, N // P, S], F32, name="staged")
+        staged = keep.tile([P, N // P, S], F32, name="staged", align_bytes=ALIGN)
         freed = {(LAST, 0): "low1", (LAST, 1): "high", (THIRD, 1): "low0"}
         o_bank = {}
 
@@ -217,8 +218,8 @@ def tile_picked_posadd_none_p_kernel(tc, x_words, x_scales, w1, w2_words, w2_sca
             )
 
         def multiply_chunk(c):
-            h_codes = keep.tile([P, CHUNK], U32, name=f"h_codes{c}", align_bytes=64)
-            h_plane = keep.tile([P, CHUNK], U8, name=f"h_plane{c}", align_bytes=64)
+            h_codes = keep.tile([P, CHUNK], U32, name=f"h_codes{c}", align_bytes=ALIGN)
+            h_plane = keep.tile([P, CHUNK], U8, name=f"h_plane{c}", align_bytes=ALIGN)
             nc.vector.quantize_mx(out=h_codes[:].bitcast(FP8X4), scales=h_plane[:], in_=h_bf[c][:])
             for a in range(N // P):
                 o_bank[c, a] = psum.tile([P, CHUNK], F32, name=f"o_bank{c}{a}", tag=freed.get((c, a), f"o_bank{c}{a}"))[:]

@@ -251,17 +251,6 @@ def tile_picked_posadd_none_p_kernel(tc, x_words, x_scales, w1, w2_words, w2_sca
             pick_pe(nc.scalar, 3, cols)
         for part in opening:
             add_pair(1, FIRST, part)
-        unread = psum.tile([P, 2, HALF], F32, name="unread", tag="high")
-        for z in range(PASSES):
-            nc.tensor.matmul_mx(
-                out=unread[:, z, :],
-                lhsT=w1_codes[z, 0][:, :P].bitcast(FP8X4),
-                lhsT_scale=w1_plane[z, 0][:, :P],
-                rhs=w1_codes[z, 1][:].bitcast(FP8X4),
-                rhs_scale=w1_plane[z, 1][:],
-                start=True,
-                stop=True,
-            )
         add_pair(1, SECOND)
         interleave(SECOND)
         multiply_chunk(FIRST)

from contextlib import ExitStack

import concourse.mybir as mybir

K, T, S, H, N = 1024, 1024, 512, 512, 256
FLOPS = 2 * K * H * S + 2 * H * N * S

F32 = mybir.dt.float32
BF16 = mybir.dt.bfloat16
I32 = mybir.dt.int32
U32 = mybir.dt.uint32
U16 = mybir.dt.uint16
U8 = mybir.dt.uint8
FP8X4 = mybir.dt.float8_e4m3fn_x4
FP4X4 = mybir.dt.float4_e2m1fn_x4
ADD = mybir.AluOpType.add
COPY = mybir.ActivationFunctionType.Copy

P = 128
PACK = 4
PASSES = K // (P * PACK)
HALF = H // 2
CHUNK = 128
CHUNKS = S // CHUNK
FIRST, SECOND, THIRD, LAST = range(CHUNKS)
VECTOR_ROUNDS = 40
VECTOR_ENTRIES = 64
ALIGN = 256


def tile_picked_posadd_none_p_kernel(tc, x_words, x_scales, w1, w2_words, w2_scales, pe, offs, out):
    nc = tc.nc
    with ExitStack() as ctx:
        keep = ctx.enter_context(tc.tile_pool(name="keep", bufs=1))
        psum = ctx.enter_context(tc.psum_pool(name="psum", bufs=1))

        offsets = keep.tile([P, S // 16], U16, name="offsets", align_bytes=ALIGN)
        x_table = [keep.tile([P, T], I32, name=f"x_table{z}", align_bytes=ALIGN) for z in range(PASSES)]
        xs_table = keep.tile([P, T], U8, name="xs_table", align_bytes=ALIGN)
        w1_raw = [keep.tile([P, PACK, H], F32, name=f"w1_raw{z}", align_bytes=ALIGN) for z in range(PASSES)]
        x_planes = keep.tile([P, PASSES, S], U8, name="x_planes", align_bytes=ALIGN)
        nc.vector.memset(xs_table[:].bitcast(I32), 0)
        nc.gpsimd.memset(x_planes[:].rearrange("p z c -> p (z c)").bitcast(I32), 0)

        def load_x(z):
            nc.sync.dma_start(out=x_table[z][:], in_=x_words[z].rearrange("p c r -> p (c r)").bitcast(I32))

        w1_rows = w1.rearrange("(z p j) c -> z p j c", z=PASSES, j=PACK)
        pe_rows = pe.rearrange("(p t) c -> p t c", t=PACK)

        load_x(0)
        nc.sync.dma_start(offsets[:], offs)
        nc.sync.dma_start(out=xs_table[0:P:4, :].bitcast(I32), in_=x_scales.bitcast(I32).rearrange("z q c -> q z c"))
        load_x(1)
        for z in range(PASSES):
            nc.sync.dma_start(out=w1_raw[z][:], in_=w1_rows[z])

        x_codes = [keep.tile([P, S], U32, name=f"x_codes{z}", align_bytes=ALIGN) for z in range(PASSES)]
        xs_picked = keep.tile([P, S], U8, name="xs_picked", align_bytes=ALIGN)
        pairs = [(z, u) for z in range(PASSES) for u in range(2)]
        w1_codes = {zu: keep.tile([P, HALF], U32, name="w1_codes%d%d" % zu, align_bytes=ALIGN) for zu in pairs}
        w1_plane = {zu: keep.tile([P, HALF], U8, name="w1_plane%d%d" % zu, align_bytes=ALIGN) for zu in pairs}
        grouped = {zu: keep.tile([P, HALF * PACK], BF16, name="grouped%d%d" % zu, align_bytes=ALIGN)[:] for zu in pairs}
        pe_picked = keep.tile([P, PACK, S], F32, name="pe_picked", align_bytes=ALIGN)
        h_pairs = {c: keep.tile([P, PACK * CHUNK], BF16, name=f"h_pairs{c}", align_bytes=ALIGN) for c in (SECOND, THIRD)}
        h_bf = [keep.tile([P, PACK * CHUNK], BF16, name=f"h_bf{c}", align_bytes=ALIGN) for c in range(CHUNKS)]
        chunks = [slice(CHUNK * c, CHUNK * (c + 1)) for c in range(CHUNKS)]

        def round_w1(copy, z, u, ms):
            copy(
                grouped[z, u].rearrange("p (t m j) -> p m j t", t=2, j=PACK)[:, ms],
                w1_raw[z][:].rearrange("p j (m t) -> p m j t", t=PACK)[:, ms, :, 2 * u : 2 * u + 2],
            )

        def entries(cols):
            return offsets[:, cols.start // 16 : cols.stop // 16]

        def pick_x(z):
            nc.vector.tensor_copy(x_codes[z][:], x_table[z][:].bitcast(U32).indirect(offsets[:]))

        def quantize_w1(z, u):
            nc.vector.quantize_mx(out=w1_codes[z, u][:].bitcast(FP8X4), scales=w1_plane[z, u][:], in_=grouped[z, u])

        def multiply(z, t, cols, bank, start, stop):
            chans = slice(P * (t % 2), P * (t % 2 + 1))
            nc.tensor.matmul_mx(
                out=bank,
                lhsT=w1_codes[z, t // 2][:, chans].bitcast(FP8X4),
                lhsT_scale=w1_plane[z, t // 2][:, chans],
                rhs=x_codes[z][:, cols].bitcast(FP8X4),
                rhs_scale=x_planes[:, z, cols],
                start=start,
                stop=stop,
            )

        product = {}

        def open_bank(tag, pieces):
            width = sum(cols.stop - cols.start for t, cols in pieces)
            bank = psum.tile([P, width], F32, name="bank%d_%d" % (pieces[0][0], pieces[0][1].start), tag=tag)
            placed, at = [], 0
            for t, cols in pieces:
                n = cols.stop - cols.start
                placed.append((t, cols, bank[:, at : at + n]))
                for c in range(cols.start // CHUNK, cols.stop // CHUNK):
                    lo = at + CHUNK * c - cols.start
                    product[t, c] = bank[:, lo : lo + CHUNK]
                at = at + n
            return bank, placed

        def multiply_bank(z, placed):
            for i, (t, cols, ap) in enumerate(placed):
                multiply(z, t, cols, ap, (z, i) == (0, 0), (z, i) == (PASSES - 1, len(placed) - 1))

        def pick_pe(engine, t, cols):
            window = pe_table[t][:].indirect(entries(cols))
            if engine is nc.scalar:
                nc.scalar.activation(pe_picked[:, t, cols], window, COPY)
            else:
                nc.vector.tensor_copy(pe_picked[:, t, cols], window)

        def add_pair(u, c, part=slice(0, CHUNK)):
            if c in h_pairs:
                sums = h_pairs[c][:].rearrange("p (u n e) -> p u n e", u=2, e=2)[:, u]
            else:
                sums = h_bf[c][:].rearrange("p (n t) -> p n t", t=PACK)[:, :, 2 * u : 2 * u + 2]
            nc.vector.tensor_tensor(
                sums[:, part],
                pair_product[u, c].rearrange("p e n -> p n e")[:, part],
                pe_picked[:, 2 * u : 2 * u + 2, chunks[c]].rearrange("p e n -> p n e")[:, part],
                ADD,
            )

        list_halves = [slice(0, S // 2), slice(S // 2, S)]
        pair_product = {}

        def open_pair_bank(tag, u, cols):
            bank, placed = open_bank(tag, [(t, cols) for t in (2 * u, 2 * u + 1)])
            for c in range(cols.start // CHUNK, cols.stop // CHUNK):
                lo = CHUNK * c - cols.start
                pair_product[u, c] = bank[:].rearrange("p (e n) -> p e n", e=2)[:, :, lo : lo + CHUNK]
            return placed

        def multiply_late(tag, cols):
            placed = open_pair_bank(tag, 1, cols)
            for z in range(PASSES):
                multiply_bank(z, placed)

        early = {
            0: [open_pair_bank("low1", 0, list_halves[1]), open_pair_bank("low0", 0, list_halves[0])],
            1: [open_pair_bank("high", 1, chunks[FIRST])],
        }

        pick_x(0)
        nc.vector.tensor_copy(xs_picked[:], xs_table[:].indirect(offsets[:]))
        for q in range(4):
            nc.sync.dma_start(
                out=x_planes[32 * q : 32 * q + 4].rearrange("p z c -> p (z c)").bitcast(I32),
                in_=xs_picked[32 * q : 32 * (q + 1) : 4, :].bitcast(I32),
            )
        pe_table = []

        def load_pe(tag):
            t = len(pe_table)
            pe_table.append(keep.tile([P, T], F32, name=f"pe_table{t}", tag=tag, align_bytes=ALIGN))
            nc.sync.dma_start(out=pe_table[t][:], in_=pe_rows[:, t, :])

        load_pe("xs_table")
        pick_x(1)
        load_pe("x_table1")
        for z in range(PASSES):
            shared = VECTOR_ROUNDS if z == PASSES - 1 else 0
            round_w1(nc.vector.tensor_copy, z, 0, slice(0, P))
            round_w1(nc.scalar.copy, z, 1, slice(shared, P))
            if shared:
                round_w1(nc.vector.tensor_copy, z, 1, slice(0, shared))
            for u in range(2):
                quantize_w1(z, u)
                if z == 0:
                    load_pe(f"grouped0{u}")
                for placed in early[u]:
                    multiply_bank(z, placed)
        w2_codes = keep.tile([P, 2 * N], U8, name="w2_codes", tag="grouped10", align_bytes=ALIGN)
        w2_plane = keep.tile([P, N], U8, name="w2_plane", tag="grouped11", align_bytes=ALIGN)
        nc.sync.dma_start(out=w2_codes[:].bitcast(I32), in_=w2_words[0].bitcast(I32))
        nc.gpsimd.memset(w2_plane[:].bitcast(I32), 0)
        for q in range(4):
            nc.sync.dma_start(
                out=w2_plane[32 * q : 32 * q + 4, :].bitcast(I32),
                in_=w2_scales[0, 4 * q : 4 * q + 4, :].bitcast(I32),
            )

        pick_pe(nc.scalar, 0, slice(0, S - CHUNK))
        pick_pe(nc.vector, 0, chunks[LAST])
        pick_pe(nc.vector, 1, chunks[LAST])
        pick_pe(nc.vector, 1, slice(S - CHUNK - VECTOR_ENTRIES, S - CHUNK))
        for cols in (slice(2 * CHUNK, S - CHUNK - VECTOR_ENTRIES), chunks[0], chunks[1]):
            pick_pe(nc.scalar, 1, cols)
        for c in (LAST, THIRD):
            add_pair(0, c)
        multiply_late("low1", chunks[SECOND])
        for c in (FIRST, SECOND):
            add_pair(0, c)
        multiply_late("low0", list_halves[1])

        pick_pe(nc.scalar, 2, slice(0, S - CHUNK))
        pick_pe(nc.vector, 2, chunks[LAST])

        out_rows = out.rearrange("(a p) n -> p a n", p=P)
        staged = keep.tile([P, N // P, S], F32, name="staged", align_bytes=ALIGN)
        freed = {(LAST, 0): "low1", (LAST, 1): "high", (THIRD, 1): "low0"}
        o_bank = {}

        def interleave(c):
            nc.scalar.copy(
                h_bf[c][:].bitcast(U32).rearrange("p (n u) -> p n u", u=2),
                h_pairs[c][:].bitcast(U32).rearrange("p (u n) -> p n u", u=2),
            )

        def multiply_chunk(c):
            h_codes = keep.tile([P, CHUNK], U32, name=f"h_codes{c}", align_bytes=ALIGN)
            h_plane = keep.tile([P, CHUNK], U8, name=f"h_plane{c}", align_bytes=ALIGN)
            nc.vector.quantize_mx(out=h_codes[:].bitcast(FP8X4), scales=h_plane[:], in_=h_bf[c][:])
            for a in range(N // P):
                o_bank[c, a] = psum.tile([P, CHUNK], F32, name=f"o_bank{c}{a}", tag=freed.get((c, a), f"o_bank{c}{a}"))[:]
                nc.tensor.matmul_mx(
                    out=o_bank[c, a],
                    lhsT=w2_codes[:, 2 * P * a : 2 * P * (a + 1)].bitcast(FP4X4),
                    lhsT_scale=w2_plane[:, P * a : P * (a + 1)],
                    rhs=h_codes[:].bitcast(FP8X4),
                    rhs_scale=h_plane[:],
                    start=True,
                    stop=True,
                )

        def store_halves(c, copies):
            for a, copy in enumerate(copies):
                copy(staged[:, a, chunks[c]], o_bank[c, a])
                nc.sync.dma_start(out=out_rows[:, a, chunks[c]], in_=staged[:, a, chunks[c]])

        def store_shared(group):
            for c in reversed(group):
                nc.scalar.copy(staged[:, 0, chunks[c]], o_bank[c, 0])
                nc.vector.tensor_copy(staged[:, 1, chunks[c]], o_bank[c, 1])
            cols = slice(chunks[group[0]].start, chunks[group[-1]].stop)
            nc.sync.dma_start(out=out_rows[:, :, cols], in_=staged[:, :, cols])

        opening = [slice(0, CHUNK // 2), slice(CHUNK // 2, CHUNK)]
        pick_pe(nc.vector, 3, slice(2 * CHUNK - VECTOR_ENTRIES, 2 * CHUNK))
        for cols in opening + [slice(CHUNK, 2 * CHUNK - VECTOR_ENTRIES)] + chunks[2:]:
            pick_pe(nc.scalar, 3, cols)
        for part in opening:
            add_pair(1, FIRST, part)
        add_pair(1, SECOND)
        interleave(SECOND)
        multiply_chunk(FIRST)
        add_pair(1, THIRD)
        interleave(THIRD)
        add_pair(1, LAST)
        for c in (SECOND, LAST, THIRD):
            multiply_chunk(c)
        store_halves(FIRST, [nc.scalar.copy, nc.scalar.copy])
        store_halves(SECOND, [nc.scalar.copy, nc.vector.tensor_copy])
        store_shared([THIRD, LAST])
